import numpy as np, ml_dtypes
CORES = [23,119,17,113]
N = 4
BF = ml_dtypes.bfloat16
def gentries(a):
    return np.ascontiguousarray(a.reshape(8, 16, -1).transpose(0, 2, 1)).reshape(8, -1)
def gtable(e):
    e = np.asarray(e); return np.ascontiguousarray(e.reshape(8, -1, 16).transpose(0, 2, 1)).reshape(128, -1).astype(np.int32)
W, MA, J, P, T = 3072, 256, 768, 4, 3
def lanes(rng, big=False):
    jm = np.zeros((N, 8, MA), np.int64); lab = np.zeros((N, 8, J), np.int64); nx = np.zeros((N, 8, 16, J), np.int64)
    for q in range(N):
        for g in range(8):
            o = rng.permutation(J); p = rng.permutation(MA)
            tail = p[(MA * rng.random(J - MA) ** 2).astype(np.int64)]
            if big: tail[:] = p[0]
            lb = np.concatenate([np.arange(MA), tail]); s = np.argsort(lb, kind="stable"); cnt = np.bincount(lb, minlength=MA); st = np.add.accumulate(cnt) - cnt
            jm[q, g] = o[:MA]; lab[q, g, o] = lb
            nx[q, g][:, o] = o[s[st[lb] + (cnt[lb] * rng.random((16, J))).astype(np.int64)]]
            if big:
                pos = np.zeros(J, np.int64); pos[s] = np.arange(J) - st[lb[s]]
                nx[q, g][:8, o] = o[s[st[lb] + (pos + 1) % cnt[lb]]]
    return jm, lab, nx
def parts(rng, big=False):
    jm, lab, nx = lanes(rng, big); pal = rng.integers(0, W, (8, 16, MA, 6))
    ga = np.arange(8)[None, :, None, None]; ka = np.arange(16)[None, None, :, None]
    tool = np.where(rng.random((N, 8, 16, J)) < 0.75, pal[ga, ka, lab[:, :, None, :], rng.integers(0, 6, (N, 8, 16, J))], rng.integers(0, W, (N, 8, 16, J)))
    sh = (N, 8, 16, P, MA)
    name = np.where(rng.random(sh) < 0.8, pal[ga[..., None], ka[..., None], np.arange(MA), rng.integers(0, 6, sh)], rng.integers(0, W, sh))
    x = np.clip(rng.integers(0, 256, (N, 8, 1, W)) + rng.integers(-64, 65, (N, 8, 16, W)), 0, 255)
    lm = np.clip(rng.integers(64, 257, (N, 8, 1, J)) + rng.integers(-48, 49, (N, 8, 16, J)), 0, 255)
    return {"jm": jm, "nx": nx, "tool": tool, "name": name, "f": rng.integers(0, J, sh), "x": x, "lm": lm, "sd": rng.integers(0, 256, (N, 8, 16, W)), "rt": rng.integers(0, 65, (N, 8, 16, T))}
def full(a):
    return np.ascontiguousarray(a.reshape(N, 128, -1))
def pack(v):
    b = {k: full(v[k]).astype(np.float32).astype(BF) for k in ("x", "sd", "lm", "rt")}
    return {"xw": b["x"], "sd": b["sd"], "jt": full(4096 * v["nx"] + v["tool"]).astype(np.int32), "lm": b["lm"], "rt": b["rt"],
            "pk": full(4096 * v["f"] + v["name"]).astype(np.int32), "jm": np.stack([gtable(a) for a in v["jm"]])}
def setup_inputs(rng):
    return pack(parts(rng))
def setup_inputs_ties(rng):
    v = parts(rng)
    n = rng.choice(np.array([0, 7, 8, 9, 10, 16]), (N, 8, 1, W)); r = np.argsort(rng.random((N, 8, 16, W)), axis=2)
    v["x"] = 100 + (r < n).astype(np.int64); v["lm"] = np.full((N, 8, 16, J), 100); v["rt"] = rng.integers(0, 3, (N, 8, 16, T))
    v["f"] = rng.choice(np.array([0, J // 2, J - 1]), (N, 8, 16, P, MA))
    v["name"][:, :, :, 1] = np.where(rng.random((N, 8, 16, MA)) < 0.5, v["name"][:, :, :, 0], v["name"][:, :, :, 1])
    return pack(v)
def setup_inputs_crowd(rng):
    v = parts(rng); few = rng.integers(0, W, (8, 24)); ga = np.arange(8)[None, :, None, None]; m = np.arange(MA)
    v["tool"] = few[ga, rng.integers(0, 24, (N, 8, 16, J))]; v["name"] = few[ga[..., None], rng.integers(0, 24, (N, 8, 16, P, MA))]
    v["x"] = rng.choice(np.array([0, 3, 7, 8, 9, 128, 250, 254, 255]), (N, 8, 16, W)); v["rt"] = rng.choice(np.array([0, 1, 5, 64]), (N, 8, 16, T))
    other = np.setdiff1d(np.arange(W), few)
    for q in range(N):
        o = rng.permutation(8)
        g = o[0]; c, d = rng.permutation(other)[:2]
        v["lm"][q, g] = 255; v["tool"][q, g] = d; v["name"][q, g] = c; v["f"][q, g][:, 0] = J - 1; v["x"][q, g][:, c] = rng.integers(32, 256, 16)
        for g, w in ((o[1], 0), (o[2], 255)):
            c, d, e = rng.permutation(other)[:3]; m0 = int(rng.integers(1, 9))
            nm = np.where(m < m0, e, c); goes = (m == m0) == (w == 0)
            v["lm"][q, g] = 255; v["x"][q, g] = w; v["name"][q, g][0] = nm
            v["tool"][q, g][0, v["jm"][q, g]] = np.where(goes, nm, d)
            v["rt"][q, g] = rng.integers(17, 65, (16, T)) if w == 0 else rng.integers(0, 3, (16, T))
        g = o[3]; a = rng.permutation(W)[:17]; k0 = rng.integers(1, 8, MA)
        v["x"][q, g][:, a[0]] = rng.integers(0, 150, 16)
        v["x"][q, g][:, a[1:]] = rng.permuted(np.tile(rng.integers(150, 256, (16, 1)), (1, 16)), axis=0)
        v["tool"][q, g][:, v["jm"][q, g]] = np.where(np.arange(16)[:, None] < k0[None, :], a[0], a[1:][:, None])
    return pack(v)
def setup_inputs_ends(rng):
    v = parts(rng, True); e = np.array([0, 1, W - 2, W - 1])
    v["tool"] = np.where(rng.random((N, 8, 16, J)) < 0.5, rng.choice(e, (N, 8, 16, J)), v["tool"])
    v["name"] = np.where(rng.random((N, 8, 16, P, MA)) < 0.5, rng.choice(e, (N, 8, 16, P, MA)), v["name"])
    v["sd"] = np.where(rng.random((N, 8, 16, W)) < 0.5, rng.choice(np.array([0, 1, 255]), (N, 8, 16, W)), v["sd"])
    v["f"] = np.where(rng.random((N, 8, 16, P, MA)) < 0.5, rng.choice(np.array([0, J - 1]), (N, 8, 16, P, MA)), v["f"])
    return pack(v)
def setup_inputs_calm(rng):
    v = parts(rng); q = rng.permutation(N)
    v["lm"][q[0]] = 255; a = np.take_along_axis(v["tool"][q[0]], v["jm"][q[0]][:, None, :], 2)
    np.put_along_axis(v["name"][q[0]], rng.integers(0, P, (8, 16, 1, MA)), a[:, :, None, :], 2)
    v["lm"][q[1]] = 0; v["x"][q[1]] = np.maximum(v["x"][q[1]], 1)
    v["tool"][q[2]] = 2 * (v["tool"][q[2]] // 2); v["sd"][q[2]] = 2 * (v["sd"][q[2]] // 2); v["name"][q[2]] = 2 * (v["name"][q[2]] // 2) + 1
    return pack(v)
def setup_inputs_spread(rng):
    v = parts(rng)
    v["x"] = np.minimum((np.exp2(8 * rng.random((N, 8, 1, W))) * rng.random((N, 8, 16, W))).astype(np.int64), 255)
    v["lm"] = np.minimum((np.exp2(8 * rng.random((N, 8, 1, J))) * rng.random((N, 8, 16, J))).astype(np.int64), 255)
    v["rt"] = np.minimum(np.exp2(6 * rng.random((N, 8, 16, T))).astype(np.int64), 64)
    v["sd"] = np.minimum(np.exp2(8 * rng.random((N, 8, 16, W))).astype(np.int64), 255)
    v["tool"] = np.where(rng.random((N, 8, 16, J)) < 0.5, np.minimum((W * rng.random((N, 8, 16, J)) ** 3).astype(np.int64), W - 1), v["tool"])
    v["f"] = np.minimum((J * rng.random((N, 8, 16, P, MA)) ** 3).astype(np.int64), J - 1)
    return pack(v)
def check_inputs(d):
    bad = []
    for k, hi in (("xw", 255), ("sd", 255), ("lm", 255), ("rt", 64)):
        v = np.asarray(d[k]).astype(np.float64)
        if not np.all((v >= 0) & (v <= hi) & (v == np.floor(v))): bad.append("range of " + k)
    for k in ("jt", "pk"):
        v = np.asarray(d[k]).astype(np.int64)
        if np.min(v) < 0 or np.max(v) > 4096 * J - 1 or np.max(v & 4095) > W - 1: bad.append("range of " + k)
    if np.min(d["jm"]) < 0 or np.max(d["jm"]) > J - 1: bad.append("range of jm")
    if bad: return bad
    ok = True; nx = np.asarray(d["jt"]).astype(np.int64).reshape(N, 8, 16, J) >> 12
    for q in range(N):
        starts = gentries(np.asarray(d["jm"][q])).astype(np.int64)
        for g in range(8):
            fr = starts[g]; lab = np.full(J, -1)
            if len(np.unique(fr)) < MA: ok = False; continue
            lab[fr] = np.arange(MA)
            while len(fr):
                tg = nx[q, g][:, fr].reshape(-1); lb = np.tile(lab[fr], 16); new = lab[tg] < 0
                lab[tg[new]] = lb[new]
                if np.any(lab[tg] != lb): ok = False; break
                fr = np.unique(tg[new])
    if not ok: bad.append("lanes: a job can be reached from the starting jobs of two machines")
    return bad
def reference(xw, sd, jt, lm, rt, pk, jm):
    x = xw.astype(np.int64).reshape(N, 8, 16, W); s = sd.astype(np.int64).reshape(N, 8, 16, W); lim = lm.astype(np.int64).reshape(N, 8, 16, J); wr = rt.astype(np.int64).reshape(N, 8, 16, T)
    tab = jt.astype(np.int64).reshape(N, 8, 16, J); p = pk.astype(np.int64).reshape(N, 8, 16, P, MA)
    j = np.stack([gentries(a) for a in jm]).astype(np.int64)
    qa = np.arange(N)[:, None, None]; ga = np.arange(8)[None, :, None]
    for t in range(T):
        jj = np.ascontiguousarray(np.broadcast_to(j[:, :, None, :], (N, 8, 16, MA)))
        rec = np.take_along_axis(tab, jj, 3); a = rec & 4095; n = rec >> 12
        xa = np.take_along_axis(x, a.reshape(N, 8, 1, 16 * MA), 3).reshape(N, 8, 16, 16, MA)
        over = xa > np.take_along_axis(lim, jj, 3)[:, :, :, None, :]
        cond = np.add.reduce(over.astype(np.int64), axis=2) >= 9
        ks = np.argmax(np.add.reduce(xa, axis=2), axis=2)[:, :, None]
        b = a + np.take_along_axis(s, a, 3); b = np.where(b >= W, b - W, b)
        n2 = np.take_along_axis(tab, n, 3) >> 12
        a = np.where(cond, b, a); n = np.where(cond, n2, n)
        np.put_along_axis(tab, jj, 4096 * n + a, 3)
        eq = (p & 4095) == a[:, :, :, None]; hit = np.any(eq, axis=3)
        slot = np.where(hit, np.argmax(eq, axis=3), np.argmax(p >> 12, axis=3))[:, :, :, None]
        old = np.take_along_axis(p, slot, 3)[:, :, :, 0]
        send = np.where(hit, p[:, :, :, P - 1], old)
        np.put_along_axis(p, slot, (4096 * n + a)[:, :, :, None], 3)
        p[:, :, :, P - 1] = np.roll(send, 1, axis=0)
        v = np.take_along_axis(np.where(hit, a, old & 4095), ks, 2)[:, :, 0]; up = np.take_along_axis(hit, ks, 2)[:, :, 0]
        j = np.take_along_axis(n, ks, 2)[:, :, 0]
        low = np.full((N, 8, W), MA); np.minimum.at(low, (qa, ga, v), np.arange(MA)[None, None, :])
        wears = np.take_along_axis(up, np.minimum(low, MA - 1), 2)[:, :, None]
        x = np.where((low < MA)[:, :, None], np.where(wears, np.minimum(x + wr[:, :, :, t:t + 1], 255), np.maximum(x - 8, 0)), x)
    return {"yx": x.reshape(N, 128, W).astype(np.float32).astype(BF), "yp": p.reshape(N, 128, P * MA).astype(np.float32)}

@@ -1,0 +1,521 @@
+from concourse.mybir import AluOpType, ActivationFunctionType
+
+OP = AluOpType
+AF = ActivationFunctionType
+KDS = (12, 10, 10)
+XV = ((2, 3), (), ())
+FL = (3, 4)
+NB = 3
+BIG = 16777216.0
+
+
+def _s(shape, names, dtype, where="sbuf"):
+    return {n: (where, shape, dtype) for n in names.split()}
+
+
+SCRATCH = {}
+SCRATCH.update(_s([128, 3328], "X", "bfloat16"))
+SCRATCH.update(_s([128, 3072], "SD", "bfloat16"))
+SCRATCH.update(_s([128, 768], "JT TT NT", "int32"))
+SCRATCH.update(_s([128, 768], "LM GI SL", "bfloat16"))
+SCRATCH.update(_s([128, 768], "OUTP", "float32"))
+SCRATCH.update(_s([128, 4], "RT", "bfloat16"))
+SCRATCH.update(_s([128, 4], "RTF THR", "float32"))
+SCRATCH.update(_s([128, 8], "BB", "float32"))
+SCRATCH.update(_s([128, 8], "ROW8 IB", "bfloat16"))
+SCRATCH.update(_s([128, 1], "HB EB", "float32"))
+SCRATCH.update(_s([128, 16], "JM PI KI PG PQ", "int32"))
+SCRATCH.update(_s([128, 16], "J0 J1 VL OL", "uint16"))
+SCRATCH.update(_s([128, 16], "VLF PF CK KM", "float32"))
+SCRATCH.update(_s([128, 1024], "PK Q M SH", "int32"))
+SCRATCH.update(_s([128, 1024], "EQ", "bfloat16"))
+SCRATCH.update(_s([128, 4096], "XG GD OV E", "bfloat16"))
+SCRATCH.update(_s([128, 4096], "GN", "float16"))
+SCRATCH.update(_s([128, 256], "A16 N16", "uint16"))
+SCRATCH.update(_s([128, 256], "AC0 AC1 TA NF0 NF1 CD CN NH MC G1 G2 G3 VR OF", "float16"))
+SCRATCH.update(_s([128, 256], "LJ HT H COND CW HH Y1 Y2 UP YT C255 BIAS RST CP CN2 CQ", "bfloat16"))
+SCRATCH.update(_s([128, 256], "PM NN UU UC SB2 LAND3 YM CM", "float32"))
+SCRATCH.update(_s([128, 256], "EV IX ME S1 S2 SB0 SB1 LAND1 LAND2", "int32"))
+SCRATCH.update(_s([128, 128], "ROWC ID NID ID8 NID16 IDQ IDM IDW BLK NBLK BLKQ ONES", "bfloat16"))
+SCRATCH.update(_s([128, 16, 128], "SEL ONE LT", "bfloat16"))
+SCRATCH.update(_s([128, 512], "b0 b1 b2 b3 b4 b5 b6 b7", "float32", "psum"))
+DMAS = ["jt", "jm", "lm", "xw", "sd", "rt", "pk", "oq", "o3", "ox"]
+SEMAPHORES = ["sv", "sa", "st", "sg"] + ["d" + d for d in DMAS] + ["ar0", "ar1", "ar2", "lc0", "lc1", "lc2"]
+PSUM = ("b0", "b1", "b2", "b3", "b4", "b5", "b6", "b7")
+
+
+def rank_program(g, core, T, topo):
+    rank = T.rank_of(core)
+    if rank is None:
+        return
+    nxt = T.cores[(rank + 1) % len(T.cores)]
+    prv = T.cores[(rank - 1) % len(T.cores)]
+    queue = {"v": g.vector, "a": g.scalar, "t": g.tensor, "g": g, "s": g.sync}
+    count = {"sv": 0, "sa": 0, "st": 0, "sg": 0}
+    seen, wrote, readers = {}, {}, {}
+
+    def emit(q, fn, R, W, sem=None, inc=1, total=None):
+        need = {}
+
+        def want(s, v):
+            if s == "st" and q == "t":
+                return
+            if need.get(s, 0) < v:
+                need[s] = v
+        own = "s" + q
+        for tag in R:
+            if tag in wrote:
+                want(*wrote[tag])
+            if tag in PSUM:
+                for s, v in readers.get(tag, {}).items():
+                    if s != own:
+                        want(s, v)
+        for tag in W:
+            if tag in wrote:
+                want(*wrote[tag])
+            for s, v in readers.get(tag, {}).items():
+                want(s, v)
+        for s in sorted(need):
+            if seen.get((q, s), 0) < need[s]:
+                queue[q].wait_ge(T.sem[s], need[s])
+                seen[(q, s)] = need[s]
+        ins = fn()
+        if sem is None:
+            sem = own
+            count[sem] += 1
+            total = count[sem]
+        if inc:
+            ins.then_inc(T.sem[sem], inc)
+        for tag in R:
+            readers.setdefault(tag, {})[sem] = total
+        for tag in W:
+            wrote[tag] = (sem, total)
+            readers[tag] = {}
+
+    def V(R, W, fn):
+        emit("v", fn, R.split(), W.split())
+
+    def D(q, name, R, W, out, in_):
+        emit(q, lambda: queue[q].dma_start(out=out, in_=in_), R.split(), W.split(), "d" + name, 16, 16)
+
+    def act(R, W, out, in_, func=AF.Copy, **kw):
+        emit("a", lambda: g.scalar.activation(out=out, in_=in_, func=func, **kw), R.split(), W.split())
+
+    def mm(R, W, out, lhsT, rhs, start, stop):
+        emit("t", lambda: g.tensor.matmul(out=out, lhsT=lhsT, rhs=rhs, start=start, stop=stop), R.split(), W.split())
+
+    def cp(R, W, out, in_):
+        V(R, W, lambda: g.vector.tensor_copy(out=out, in_=in_))
+
+    def tt(R, W, out, in0, in1, op):
+        V(R, W, lambda: g.vector.tensor_tensor(out=out, in0=in0, in1=in1, op=op))
+
+    def ts(R, W, out, in0, s1, op0, s2=None, op1=None):
+        if op1 is None:
+            V(R, W, lambda: g.vector.tensor_scalar(out=out, in0=in0, scalar1=s1, scalar2=None, op0=op0))
+        else:
+            V(R, W, lambda: g.vector.tensor_scalar(out=out, in0=in0, scalar1=s1, scalar2=s2, op0=op0, op1=op1))
+
+    def fill(W, ap, c):
+        V("", W, lambda: g.vector.memset(ap, c))
+
+    def lo(b):
+        return b[:, 0:256]
+
+    def hi(b):
+        return b[:, 256:512]
+
+    D("s", "jt", "", "JT", T.JT[:], T.jt[:])
+    D("a", "jm", "", "JM", T.JM[:], T.jm[:])
+    D("s", "sd", "", "SD", T.SD[:], T.sd[:])
+    D("a", "xw", "", "X", T.X[:, 0:3072], T.xw[:])
+    D("a", "lm", "", "LM", T.LM[:], T.lm[:])
+    D("s", "pk", "", "PK", T.PK[:], T.pk[:])
+    D("s", "rt", "", "RT", T.RT[:, 0:3], T.rt[:])
+
+    def iota(nm, pattern, base=0, cm=0, exact=True):
+        if exact:
+            emit("g", lambda: g.iota(T[nm][:], pattern, base, cm), [], [nm])
+        else:
+            emit("g", lambda: g.iota(T[nm][:], pattern, base, cm, allow_small_or_imprecise_dtypes=True), [], [nm])
+
+    def select(nm, pattern, op, base, cm):
+        emit("g", lambda: g.affine_select(T[nm][:], T[nm][:], pattern, op, 0.0, base, cm), [nm], [nm])
+    iota("PI", [[0, 16]], 0, 1)
+    iota("KI", [[1, 16]])
+    iota("ROWC", [[1, 128]], exact=False)
+    iota("ROW8", [[16, 8]], exact=False)
+    iota("BIAS", [[0, 16], [-1, 16]], 15, exact=False)
+    iota("RST", [[0, 256]], 1, exact=False)
+    select("RST", [[0, 16], [1, 16]], OP.not_equal, 0, 0)
+    iota("CP", [[0, 256]], 1664, exact=False)
+    blocks = [[0, 16], [0, 8], [0, 16]]
+    iota("ONE", blocks, 1, exact=False)
+    select("ONE", [[-1, 16], [0, 8], [1, 16]], OP.is_equal, 0, 0)
+    select("ONE", [[0, 16], [-16, 8], [0, 16]], OP.is_ge, 0, 1)
+    select("ONE", [[0, 16], [16, 8], [0, 16]], OP.is_ge, 15, -1)
+    for nm, x in (("BLK", 1), ("NBLK", -1), ("BLKQ", 4096)):
+        iota(nm, [[0, 128]], x, exact=False)
+        select(nm, [[-16, 8], [0, 16]], OP.is_ge, 0, 1)
+        select(nm, [[16, 8], [0, 16]], OP.is_ge, 15, -1)
+    iota("LT", blocks, 4096, exact=False)
+    select("LT", [[0, 16], [-16, 8], [0, 16]], OP.is_ge, 0, 1)
+    select("LT", [[1, 16], [16, 8], [0, 16]], OP.is_ge, -1, -1)
+    iota("CQ", [[0, 256]], -2048, exact=False)
+    iota("C255", [[0, 256]], 255, exact=False)
+    iota("CM", [[1, 256]], 1408, exact=False)
+    fill("CN2", T.CN2[:], -1664.0)
+    fill("HB", T.HB[:], -0.5)
+    fill("EB", T.EB[:], -8.0)
+    fill("ONES", T.ONES[:], 1.0 / 128)
+    for i, x in enumerate((12288.0, 8192.0, 4096.0, -1664.0, BIG)):
+        fill("BB", T.BB[:, i:i + 1], x)
+    cp("PI", "PF", T.PF[:], T.PI[:])
+    ts("ROWC PF", "ID", T.ID[:], T.ROWC[:], T.PF[:, 0:1], OP.is_equal)
+    ts("PI", "PQ", T.PQ[:], T.PI[:], 15, OP.bitwise_and)
+    tt("PQ KI", "KM", T.KM[:], T.PQ[:], T.KI[:], OP.is_equal)
+    for k in range(16):
+        ts("ID KM", "SEL", T.SEL[:, k, :], T.ID[:], T.KM[:, k:k + 1], OP.mult)
+
+    def gather_tools(t):
+        J = "J%d" % (t % 2)
+        cp("TT " + J, "A16", T.A16[:], T.TT[:].indirect(T[J][:]))
+
+    def gather_jobs(t):
+        J = "J%d" % (t % 2)
+        ac, nf = "AC%d" % (t % 2), "NF%d" % (t % 2)
+        if t == 0:
+            ts("JT", "NT", T.NT[:], T.JT[:], 12, OP.logical_shift_right)
+        cp("NT " + J, "N16", T.N16[:], T.NT[:].indirect(T[J][:]))
+        if t:
+            act("LM " + J, "LJ", T.LJ[:], T.LM[:].indirect(T[J][:]))
+        ts("A16", "TA", T.TA[:], T.A16[:], -1.0, OP.mult, 1408.0, OP.add)
+        ts("A16", ac, T[ac][:], T.A16[:], -1664.0, OP.add)
+        cp("N16", nf, T[nf][:], T.N16[:])
+
+    defer, dd, held = [], [], []
+
+    def flush_d():
+        while dd:
+            dd.pop(0)()
+
+    def flush():
+        if defer:
+            defer.pop(0)()
+
+    def gather_d(c):
+        w = slice(1024 * c, 1024 * c + 1024)
+        s = slice(64 * c, 64 * c + 64)
+        act("SD A16", "GD%d" % c, T.GD[:, w], T.SD[:].indirect(T.A16[:, s]))
+
+        def later():
+            for k in range(16):
+                mm("GD%d SEL" % c, "b3", T.b3[:, s], T.SEL[:, k, :], T.GD[:, w.start + k:w.stop:16], k == 0, False)
+            mm("ID CN2", "b3", T.b3[:, s], T.ID[:], T.CN2[:, s], False, True)
+        dd.append(later)
+
+    def gather_n(c, t):
+        nf = "NF%d" % (t % 2)
+        w = slice(1024 * c, 1024 * c + 1024)
+        s = slice(64 * c, 64 * c + 64)
+        cp("NT N16", "GN%d" % c, T.GN[:, w], T.NT[:].indirect(T.N16[:, s]))
+
+        def later():
+            o = T.b3[:, 256 + 64 * c:320 + 64 * c]
+            for k in range(16):
+                mm("GN%d SEL" % c, "b3", o, T.SEL[:, k, :], T.GN[:, w.start + k:w.stop:16], k == 0, False)
+            mm("NID " + nf, "b3", o, T.NID[:], T[nf][:, s], False, True)
+        defer.append(later)
+
+    def sums(h):
+        for k in range(16):
+            mm("XG%d XG%d IB" % (2 * h, 2 * h + 1), "b4", T.b4[:, 128 * h + k:128 * h + 128:16], T.XG[:, 2048 * h + k:2048 * h + 2048:16],
+               T.IB[:], False, h == 1 and k == 15)
+
+    def heavy():
+        V("RST b4", "PM", lambda: g.vector.tensor_tensor_scan(out=T.PM[:], data0=T.RST[:], data1=lo(T.b4), initial=0.0, op0=OP.mult, op1=OP.max))
+        cp("PM", "PM", T.PM[:, 7::16], T.PM[:, 15::16])
+        cp("PM", "PM", T.PM[:, 3::8], T.PM[:, 7::8])
+        cp("PM", "PM", T.PM[:, 1::4], T.PM[:, 3::4])
+        cp("PM", "PM", T.PM[:, 0::2], T.PM[:, 1::2])
+        tt("b4 PM", "HT", T.HT[:], lo(T.b4), T.PM[:], OP.is_equal)
+        for h in range(2):
+            mm("HT ID", "b5", T.b5[:, 128 * h:128 * h + 128], T.HT[:, 128 * h:128 * h + 128], T.ID[:], True, True)
+        act("b5", "H", T.H[:], lo(T.b5))
+
+    def over_a(i):
+        b = "b%d" % (i % 2)
+        for k, o in ((2 * i, lo(T[b])), (2 * i + 1, hi(T[b]))):
+            mm("NID LJ", b, o, T.NID[:], T.LJ[:], True, False)
+            mm("XG0 XG1 XG2 XG3 ID", b, o, T.ID[:], T.XG[:, k::16], False, True)
+        act(b + " HB", "OVA%d" % i, T.OV[:, 512 * i:512 * i + 512], T[b][:], AF.Sign, bias=T.HB[:])
+
+    def count_a(i, end):
+        for k in (2 * i, 2 * i + 1):
+            mm("OVA%d ONE" % i, "b2", lo(T.b2), T.ONE[:, k, :], T.OV[:, 256 * k:256 * k + 256], k == 0, k == end)
+
+    def wear(t, fillers):
+        kd = KDS[t]
+        for c in range(4):
+            if c not in XV[t]:
+                act("X A16", "XG%d" % c, T.XG[:, 1024 * c:1024 * c + 1024], T.X[:, 0:3072].indirect(T.A16[:, 64 * c:64 * c + 64]))
+        fillers(0)
+        mm("ONES BIAS", "b4", lo(T.b4), T.ONES[:], T.BIAS[:], True, False)
+        for c in XV[t]:
+            cp("X A16", "XG%d" % c, T.XG[:, 1024 * c:1024 * c + 1024], T.X[:, 0:3072].indirect(T.A16[:, 64 * c:64 * c + 64]))
+        sums(0)
+        sums(1)
+        mm("ID LJ", "b7", lo(T.b7), T.ID[:], T.LJ[:], True, True)
+        for i in range(kd // 2):
+            over_a(i)
+            if i:
+                count_a(i - 1, 15)
+            if i == 3:
+                heavy()
+                fillers(1)
+            if i in FL:
+                flush()
+        count_a(kd // 2 - 1, 15)
+        while defer:
+            flush()
+        for k in range(kd, 16):
+            tt("XG0 XG1 XG2 XG3 b7", "OVD%d" % k, T.OV[:, 256 * k:256 * k + 256], T.XG[:, k::16], lo(T.b7), OP.is_gt)
+        for k in range(kd, 16):
+            mm("OVD%d ONE" % k, "b2", lo(T.b2), T.ONE[:, k, :], T.OV[:, 256 * k:256 * k + 256], False, k == 15)
+        fillers(2)
+
+    def list_of(R, src, o):
+        for r in range(16):
+            mm(R + " ONE", "b7", T.b7[:, o:o + 16], T.ONE[:, r, :], src[:, r::16], r == 0, r == 15)
+
+    def pocket3(t):
+        return ("Q3", T.Q[:, 768:1024]) if t == 0 else ("LAND%d" % t, T["LAND%d" % t][:])
+
+    def victims(t):
+        q3, l3 = pocket3(t)
+        tt("Q0 Q1", "b5", hi(T.b5), T.Q[:, 0:256], T.Q[:, 256:512], OP.max)
+        tt("b5 Q2", "b5", hi(T.b5), T.Q[:, 512:768], hi(T.b5), OP.max)
+        tt("b5 " + q3, "EV", T.EV[:], l3, hi(T.b5), OP.max)
+        ts("EV", "ME", T.ME[:], T.EV[:], 4095, OP.bitwise_and)
+        ts("EV", "IX", T.IX[:], T.EV[:], 12, OP.logical_shift_right, 3, OP.bitwise_and)
+        for i in range(3):
+            ts("IX", "GI%d" % i, T.GI[:, 256 * i:256 * i + 256], T.IX[:], float(3 - i), OP.is_equal)
+        ts("ME", "MC", T.MC[:], T.ME[:], -1664.0, OP.add)
+        if t:
+            ts(q3, "M3", T.M[:, 768:1024], l3, 4095, OP.bitwise_and)
+
+    def init_pockets():
+        ts("PK", "SH", T.SH[:], T.PK[:], 12, OP.logical_shift_right)
+        ts("PK", "M0 M1 M2 M3", T.M[:], T.PK[:], 4095, OP.bitwise_and)
+        for i in range(4):
+            s = slice(256 * i, 256 * i + 256)
+            ts("SH", "b6", hi(T.b6), T.SH[:, s], 12288.0, OP.mult, 4096.0 * (3 - i), OP.add)
+            tt("PK b6", "Q%d" % i, T.Q[:, s], T.PK[:, s], hi(T.b6), OP.add)
+
+    def finish_pockets():
+        ts("Q0 Q1 Q2", "SH", T.SH[:, 0:768], T.Q[:, 0:768], 14, OP.logical_shift_right)
+        for i in range(3):
+            s = slice(256 * i, 256 * i + 256)
+            b = ("b0", "b1", "b2")[i]
+            ts("SH", b, lo(T[b]), T.SH[:, s], -12288.0, OP.mult, -4096.0 * (3 - i), OP.add)
+            tt("Q%d " % i + b, "OUTP%d" % i, T.OUTP[:, s], T.Q[:, s], lo(T[b]), OP.add)
+        D("s", "oq", "OUTP0 OUTP1 OUTP2", "YP", T.yp[:, 0:768], T.OUTP[:])
+
+    def sel(i, t):
+        s = slice(256 * i, 256 * i + 256)
+        eq = [T.EQ[:, 256 * j:256 * j + 256] for j in range(4)]
+        b, o = (("b6", lo(T.b6)), ("b6", hi(T.b6)), ("b4", lo(T.b4)))[i]
+        mm("ID8 EQ%d" % i, b, o, T.ID8[:], eq[i], True, False)
+        for j in range(4):
+            if j < i:
+                mm("NID16 EQ%d" % j, b, o, T.NID16[:], eq[j], False, False)
+            elif j > i:
+                mm("NID EQ%d" % j, b, o, T.NID[:], eq[j], False, False)
+        mm("ID GI%d" % i, b, o, T.ID[:], T.GI[:, s], False, True)
+        if t == 2:
+            act(b, b, o, o, AF.Relu)
+            act(b, "SL%d" % i, T.SL[:, s], o, AF.Sign)
+        else:
+            held.append(lambda: ts(b, "SL%d" % i, T.SL[:, s], o, 0.5, OP.is_ge))
+
+    def update(t):
+        at = (("b0", lo(T.b0)), ("b0", hi(T.b0)), ("b1", lo(T.b1)))
+        for i, (b, o) in enumerate(at):
+            tt("Q%d " % i + b, b, o, o, T.Q[:, 256 * i:256 * i + 256], OP.subtract)
+        for i, (b, o) in enumerate(at):
+            s = slice(256 * i, 256 * i + 256)
+            if held:
+                held.pop(0)()
+            tt("SL%d " % i + b, b, o, T.SL[:, s], o, OP.mult)
+            tt("Q%d " % i + b, "Q%d" % i, T.Q[:, s], T.Q[:, s], o, OP.add)
+            if t < 2:
+                ts("Q%d" % i, "M%d" % i, T.M[:, s], T.Q[:, s], 4095, OP.bitwise_and)
+
+    def wrap():
+        tt("TA b3", "b4", hi(T.b4), T.TA[:], lo(T.b3), OP.is_gt)
+
+    cp("JM", "J0", T.J0[:], T.JM[:])
+    ts("JT", "TT", T.TT[:], T.JT[:], 4095, OP.bitwise_and)
+    gather_tools(0)
+    gather_jobs(0)
+    act("ID", "NID", T.NID[:], T.ID[:], scale=-1.0)
+    for c in range(4):
+        gather_d(c)
+        flush_d()
+    act("LM J0", "LJ", T.LJ[:], T.LM[:].indirect(T.J0[:]))
+    for nm, f in (("ID8", 8.0), ("NID16", -16.0), ("IDQ", 16384.0), ("IDM", -1408.0), ("IDW", 3072.0)):
+        act("ID", nm, T[nm][:], T.ID[:], scale=f)
+
+    def first(x):
+        if x == 0:
+            for c in range(4):
+                gather_n(c, 0)
+            wrap()
+            ts("PI", "PG", T.PG[:], T.PI[:], 112, OP.bitwise_and)
+            tt("PG KI", "CK", T.CK[:], T.PG[:], T.KI[:], OP.add)
+            ts("ROW8 CK", "IB", T.IB[:], T.ROW8[:], T.CK[:, 0:1], OP.is_equal, 16.0, OP.mult)
+            ts("RT", "RTF", T.RTF[:, 0:3], T.RT[:, 0:3], -1.0, OP.mult, 255.0, OP.add)
+            for t in range(3):
+                ts("PQ", "THR", T.THR[:, t:t + 1], T.PQ[:, 0:1], KDS[t] - 0.5, OP.is_ge, 8.0, OP.mult)
+        elif x == 1:
+            init_pockets()
+        else:
+            victims(0)
+    wear(0, first)
+
+    for t in range(3):
+        last = t == 2
+        J, J2 = "J%d" % (t % 2), "J%d" % ((t + 1) % 2)
+        ac, nf = "AC%d" % (t % 2), "NF%d" % (t % 2)
+
+        def tool(b, o, first, stop):
+            mm("ID " + ac, b, o, T.ID[:], T[ac][:], first, False)
+            mm("ID CP", b, o, T.ID[:], T.CP[:], False, False)
+            mm("IDM COND", b, o, T.IDM[:], T.COND[:], False, False)
+            mm("ID CD", b, o, T.ID[:], T.CD[:], False, False)
+            mm("IDW CW", b, o, T.IDW[:], T.CW[:], False, stop)
+        ts("b2 THR", "COND", T.COND[:], lo(T.b2), T.THR[:, t:t + 1], OP.is_gt)
+        tt("COND b3", "CN", T.CN[:], T.COND[:], hi(T.b3), OP.mult)
+        mm("ID " + nf, "b6", hi(T.b6), T.ID[:], T[nf][:], True, False)
+        mm("ID CN", "b6", hi(T.b6), T.ID[:], T.CN[:], False, True)
+        act("b6", "NN", T.NN[:], hi(T.b6))
+        tt("COND b3", "CD", T.CD[:], T.COND[:], lo(T.b3), OP.mult)
+        tt("COND b4", "CW", T.CW[:], T.COND[:], hi(T.b4), OP.mult)
+        tool("b6", lo(T.b6), True, True)
+        if not last:
+            tt("NN b5", "NH", T.NH[:], T.NN[:], lo(T.b5), OP.mult)
+        tt("MC b5", "G1", T.G1[:], T.MC[:], lo(T.b5), OP.mult)
+        for i in range(4):
+            tt("M%d b6" % i, "EQ%d" % i, T.EQ[:, 256 * i:256 * i + 256], T.M[:, 256 * i:256 * i + 256], lo(T.b6), OP.is_equal)
+        act("b6 BB", "UC", T.UC[:], lo(T.b6), AF.Identity, bias=T.BB[:, 3:4])
+        if not last:
+            act("b6", "UU", T.UU[:], lo(T.b6))
+            list_of("NH", T.NH, 288)
+        for i in range(4):
+            mm("ID EQ%d" % i, "b2", hi(T.b2), T.ID[:], T.EQ[:, 256 * i:256 * i + 256], i == 0, i == 3)
+        if not last:
+            cp("b7", J2, T[J2][:], T.b7[:, 288:304])
+        tt("H b2", "b5", hi(T.b5), T.H[:], hi(T.b2), OP.min)
+        tt("MC b5", "G3", T.G3[:], T.MC[:], hi(T.b5), OP.mult)
+        tt("UC b5", "G2", T.G2[:], T.UC[:], hi(T.b5), OP.mult)
+        act("b5", "HH", T.HH[:], hi(T.b5))
+        act("b2 BB", "b2", lo(T.b2), hi(T.b2), AF.Relu, scale=-BIG, bias=T.BB[:, 4:5])
+        mm("BLK G1", "b7", lo(T.b7), T.BLK[:], T.G1[:], True, False)
+        mm("NBLK G3", "b7", lo(T.b7), T.NBLK[:], T.G3[:], False, False)
+        mm("BLK G2", "b7", lo(T.b7), T.BLK[:], T.G2[:], False, True)
+        mm("BLK HH", "b2", hi(T.b2), T.BLK[:], T.HH[:], True, True)
+        if not last:
+            cp("UU " + J, "TT", T.TT[:].indirect(T[J][:]), T.UU[:])
+        cp("b7", "VR", T.VR[:], lo(T.b7))
+        list_of("VR", T.VR, 256)
+        act("b2", "UP", T.UP[:], hi(T.b2))
+
+        def give():
+            q3, l3 = pocket3(t)
+            tt(q3 + " b2", "b2", lo(T.b2), l3, lo(T.b2), OP.max)
+            tt("EV b2", "S1", T.S1[:], T.EV[:], lo(T.b2), OP.min)
+            sb = "SB%d" % t
+            if not last:
+                ts("S1", sb, T[sb][:], T.S1[:], 0xFFCFFF, OP.bitwise_and)
+            else:
+                ts("S1", "IX", T.IX[:], T.S1[:], 14, OP.logical_shift_right)
+                ts("S1", "S2", T.S2[:], T.S1[:], 0xFFCFFF, OP.bitwise_and)
+                ts("IX", "b2", lo(T.b2), T.IX[:], -12288.0, OP.mult)
+                tt("S2 b2", sb, T[sb][:], T.S2[:], lo(T.b2), OP.add)
+            rid, pid = topo.addr(nxt)[0:2]
+            emit("g", lambda: g.remote_dma(out_ap=T["LAND%d" % (t + 1)][:], in_ap=T[sb][:], remote_sem=T.sem["ar%d" % t], local_sem=T.sem["lc%d" % t],
+                                           pid=pid, routing_id=rid, dma_engine_mask=topo.mask(core, nxt)),
+                 [sb], [], "lc%d" % t, 0, len(topo.engines(core, nxt)))
+            wrote["LAND%d" % (t + 1)] = ("ar%d" % t, len(topo.engines(prv, core)))
+        if not last:
+            gather_tools(t + 1)
+            gather_d(0)
+            cp("NN " + J, "NT", T.NT[:].indirect(T[J][:]), T.NN[:])
+        else:
+            give()
+        ts("b7", "VL", T.VL[:], T.b7[:, 256:272], 0.0625, OP.mult, 1664.0, OP.add)
+        ts("b7", "VLF", T.VLF[:], T.b7[:, 256:272], 0.0625, OP.mult)
+        for q in range(16):
+            ts("VR VLF", "E%d" % q, T.E[:, 256 * q + 16 * q:256 * q + 256], T.VR[:, 16 * q:256], T.VLF[:, q:q + 1], OP.is_equal)
+        act("X VL EB", "Y2", T.Y2[:], T.X[:, 0:3072].indirect(T.VL[:]), AF.Relu, bias=T.EB[:])
+        act("X VL RTF", "Y1", T.Y1[:], T.X[:, 0:3072].indirect(T.VL[:]), AF.Relu, scale=-1.0, bias=T.RTF[:, t:t + 1])
+        mm("IDQ " + nf, "b1", hi(T.b1), T.IDQ[:], T[nf][:], True, False)
+        mm("IDQ CN", "b1", hi(T.b1), T.IDQ[:], T.CN[:], False, False)
+        tool("b1", hi(T.b1), False, True)
+        mm("ID CQ", "b5", lo(T.b5), T.ID[:], T.CQ[:], True, False)
+        for q in range(15):
+            mm("BLKQ E%d" % q, "b5", T.b5[:, 16 * q + 16:256], T.BLKQ[:], T.E[:, 256 * q + 16 * q + 16:256 * q + 256], False, False)
+        ee = " ".join("E%d" % q for q in range(16))
+        for r in range(1, 16):
+            mm("LT " + ee, "b5", T.b5[:, r:256:16], T.LT[:, r, :], T.E[:, r::272], False, r == 15)
+        if not last:
+            give()
+        tt("CM b5", "YM", T.YM[:], T.CM[:], lo(T.b5), OP.min)
+        tt("YM b7", "OF", T.OF[:], T.YM[:], lo(T.b7), OP.max)
+        mm("ID C255", "b5", hi(T.b5), T.ID[:], T.C255[:], True, False)
+        mm("NID Y1", "b5", hi(T.b5), T.NID[:], T.Y1[:], False, False)
+        mm("NID Y2", "b5", hi(T.b5), T.NID[:], T.Y2[:], False, True)
+        list_of("OF", T.OF, 272)
+        if not last:
+            gather_jobs(t + 1)
+        tt("UP b5", "YT", T.YT[:], T.UP[:], hi(T.b5), OP.mult)
+        if not last:
+            gather_d(1)
+        for i in range(3):
+            b, o = (("b0", lo(T.b0)), ("b0", hi(T.b0)), ("b1", lo(T.b1)))[i]
+            act("b1 BB", b, o, hi(T.b1), AF.Identity, bias=T.BB[:, i:i + 1])
+        ts("b7", "OL", T.OL[:], T.b7[:, 272:288], 0.0625, OP.mult, 1664.0, OP.add)
+        V("Y2 YT OL", "X", lambda: g.vector.tensor_tensor(out=T.X[:].indirect(T.OL[:]), in0=T.Y2[:], in1=T.YT[:], op=OP.add))
+        if last:
+            D("s", "ox", "X", "YX", T.yx[:, 0:3072], T.X[:, 0:3072])
+            for i in range(3):
+                sel(i, t)
+            update(t)
+            finish_pockets()
+            D("a", "o3", "LAND3", "YP3", T.yp[:, 768:1024], T.LAND3[:])
+        else:
+            gather_d(2)
+            gather_d(3)
+
+            def fillers(x):
+                if x == 0:
+                    for i in range(3):
+                        sel(i, t)
+                    flush_d()
+                    update(t)
+                    wrap()
+                    for c in range(NB):
+                        gather_n(c, t + 1)
+                elif x == 1:
+                    for c in range(NB, 4):
+                        gather_n(c, t + 1)
+                else:
+                    victims(t + 1)
+            wear(t + 1, fillers)
+    for s in ("sv", "sa", "st", "sg"):
+        g.wait_ge(T.sem[s], count[s])
+    for d in DMAS:
+        g.wait_ge(T.sem["d" + d], 16)
+    for t in range(3):
+        g.wait_ge(T.sem["lc%d" % t], len(topo.engines(core, nxt)))
+        g.wait_ge(T.sem["ar%d" % t], len(topo.engines(prv, core)))

@@ -1,12 +1,16 @@
+from concourse.bass import DstId, RemoteDMATransfer
 from concourse.mybir import AluOpType, ActivationFunctionType
 
 OP = AluOpType
 AF = ActivationFunctionType
-KDS = (12, 10, 10)
-XV = ((2, 3), (), ())
-FL = (3, 4)
-NB = 3
 BIG = 16777216.0
+B2, A1, A2 = ((0, 1),), ((4, 5), (6, 7)), ((0, 1), (2, 3))
+B1 = (((6, 7),), ((4, 5), (6, 7)), ((4, 5), (6, 7)))
+AV = (("GD", (2, 3)),)
+SCALED = (("NID", -1.0), ("IW", -1536.0), ("IC", 1664.0), ("IK", 1024.0), ("IF", 12288.0), ("I8", 8192.0), ("I4", 4096.0), ("IB", BIG),
+          ("N4", -4096.0), ("NB", -BIG), ("IQ", 16384.0), ("IP0", 13952.0), ("IP1", 9856.0), ("IP2", 5760.0), ("NF", -12288.0), ("IL", 4194304.0), ("IM", 1048576.0))
+BIASES = (("job", 1279.625), ("key", 1279.53125), ("wrap", -1407.5), ("name", -1664.0), ("next", -2304.0), ("rec", 4195968.0), ("list", 1664.0),
+          ("rest", -8.0), ("bit", -1.5), ("s0", -2.5), ("s1", -1021.5), ("s2", -1536.5))
 
 
 def _s(shape, names, dtype, where="sbuf"):
@@ -16,28 +20,27 @@ def _s(shape, names, dtype, where="sbuf"):
 SCRATCH = {}
 SCRATCH.update(_s([128, 3328], "X", "bfloat16"))
 SCRATCH.update(_s([128, 3072], "SD", "bfloat16"))
-SCRATCH.update(_s([128, 768], "JT TT NT", "int32"))
-SCRATCH.update(_s([128, 768], "LM GI SL", "bfloat16"))
-SCRATCH.update(_s([128, 768], "OUTP", "float32"))
+SCRATCH.update(_s([128, 768], "JT", "int32"))
+SCRATCH.update(_s([128, 768], "LM SG", "bfloat16"))
+SCRATCH.update(_s([128, 768], "OUTP TQ", "float32"))
 SCRATCH.update(_s([128, 4], "RT", "bfloat16"))
-SCRATCH.update(_s([128, 4], "RTF THR", "float32"))
-SCRATCH.update(_s([128, 8], "BB", "float32"))
-SCRATCH.update(_s([128, 8], "ROW8 IB", "bfloat16"))
-SCRATCH.update(_s([128, 1], "HB EB", "float32"))
-SCRATCH.update(_s([128, 16], "JM PI KI PG PQ", "int32"))
+SCRATCH.update(_s([128, 4], "RS", "float32"))
+SCRATCH.update(_s([128, 16], "BB PF", "float32"))
+SCRATCH.update(_s([128, 8], "ROW8 GS GB", "bfloat16"))
+SCRATCH.update(_s([128, 16], "JM PI PQ", "int32"))
 SCRATCH.update(_s([128, 16], "J0 J1 VL OL", "uint16"))
-SCRATCH.update(_s([128, 16], "VLF PF CK KM", "float32"))
-SCRATCH.update(_s([128, 1024], "PK Q M SH", "int32"))
+SCRATCH.update(_s([128, 1024], "PK Q M", "int32"))
 SCRATCH.update(_s([128, 1024], "EQ", "bfloat16"))
+SCRATCH.update(_s([128, 1024], "FH", "float16"))
 SCRATCH.update(_s([128, 4096], "XG GD OV E", "bfloat16"))
 SCRATCH.update(_s([128, 4096], "GN", "float16"))
 SCRATCH.update(_s([128, 256], "A16 N16", "uint16"))
-SCRATCH.update(_s([128, 256], "AC0 AC1 TA NF0 NF1 CD CN NH MC G1 G2 G3 VR OF", "float16"))
-SCRATCH.update(_s([128, 256], "LJ HT H COND CW HH Y1 Y2 UP YT C255 BIAS RST CP CN2 CQ", "bfloat16"))
-SCRATCH.update(_s([128, 256], "PM NN UU UC SB2 LAND3 YM CM", "float32"))
-SCRATCH.update(_s([128, 256], "EV IX ME S1 S2 SB0 SB1 LAND1 LAND2", "int32"))
-SCRATCH.update(_s([128, 128], "ROWC ID NID ID8 NID16 IDQ IDM IDW BLK NBLK BLKQ ONES", "bfloat16"))
-SCRATCH.update(_s([128, 16, 128], "SEL ONE LT", "bfloat16"))
+SCRATCH.update(_s([128, 256], "AC NX CU CN UC NN NH MC G1 G2 G3 VR FE F3", "float16"))
+SCRATCH.update(_s([128, 256], "LJ WR HT H COND HH DL Y1 Y2 IXB B1 BIAS RST ROW16 MASK ONE NONE N1K", "bfloat16"))
+SCRATCH.update(_s([128, 256], "PM PX PV PO REC CM T1F T2F Q3F LAND3", "float32"))
+SCRATCH.update(_s([128, 256], "A32 EV IX ME T10 T20 T11 T21 LAND1 LAND2", "int32"))
+SCRATCH.update(_s([128, 144], "ROWC SH", "bfloat16"))
+SCRATCH.update(_s([128, 128], "ID ZERO BLK NBLK BLKQ AVG " + " ".join(n for n, _ in SCALED), "bfloat16"))
 SCRATCH.update(_s([128, 512], "b0 b1 b2 b3 b4 b5 b6 b7", "float32", "psum"))
 DMAS = ["jt", "jm", "lm", "xw", "sd", "rt", "pk", "oq", "o3", "ox"]
 SEMAPHORES = ["sv", "sa", "st", "sg"] + ["d" + d for d in DMAS] + ["ar0", "ar1", "ar2", "lc0", "lc1", "lc2"]
@@ -98,7 +101,13 @@ def rank_program(g, core, T, topo):
     def D(q, name, R, W, out, in_):
         emit(q, lambda: queue[q].dma_start(out=out, in_=in_), R.split(), W.split(), "d" + name, 16, 16)
 
-    def act(R, W, out, in_, func=AF.Copy, **kw):
+    def act(R, W, out, in_, func=AF.Copy, bias=None, **kw):
+        if bias is not None:
+            i = [n for n, _ in BIASES].index(bias)
+            kw["bias"] = T.BB[:, i:i + 1]
+            R += " BB"
+            if func == AF.Copy:
+                func = AF.Identity
         emit("a", lambda: g.scalar.activation(out=out, in_=in_, func=func, **kw), R.split(), W.split())
 
     def mm(R, W, out, lhsT, rhs, start, stop):
@@ -116,22 +125,41 @@ def rank_program(g, core, T, topo):
         else:
             V(R, W, lambda: g.vector.tensor_scalar(out=out, in0=in0, scalar1=s1, scalar2=s2, op0=op0, op1=op1))
 
+    def scan(R, W, out, d0, d1, initial, op0, op1):
+        V(R, W, lambda: g.vector.tensor_tensor_scan(out=out, data0=d0, data1=d1, initial=initial, op0=op0, op1=op1))
+
     def fill(W, ap, c):
         V("", W, lambda: g.vector.memset(ap, c))
 
-    def lo(b):
-        return b[:, 0:256]
+    def part(name, i):
+        return T[name][:, 256 * i:256 * i + 256]
 
-    def hi(b):
-        return b[:, 256:512]
+    def at(place, a=0, b=256, step=1):
+        o = 256 * "lh".index(place[2])
+        return T[place[:2]][:, o + a:o + b:step]
 
-    D("s", "jt", "", "JT", T.JT[:], T.jt[:])
+    def add(place, terms, start=False, stop=False):
+        for n, (w, x) in enumerate(terms):
+            tag, ap = (x, T[x][:]) if isinstance(x, str) else x
+            first, end = start and n == 0, stop and n == len(terms) - 1
+            if w[0] == "~":
+                for h in range(2):
+                    mm(tag + " " + w[1:], place[:2], at(place, 128 * h, 128 * h + 128), T[tag][:, 128 * h:128 * h + 128], T[w[1:]][:], False, end and h == 1)
+            else:
+                mm(tag + " " + w, place[:2], at(place), T[w][:], ap, first, end)
+
+    def pick(place, what, h, tag, rhs, stop):
+        tags = " ".join("%s%d" % (what, c) for c in range(4 * h, 4 * h + 4)) + " " + tag
+        for k in range(16):
+            mm(tags, place[:2], at(place, 128 * h + k, 128 * h + 128, 16), T[what][:, 2048 * h + k:2048 * h + 2048:16], rhs(k), False, stop and k == 15)
+
     D("a", "jm", "", "JM", T.JM[:], T.jm[:])
+    D("s", "jt", "", "JT", T.JT[:], T.jt[:])
+    D("s", "xw", "", "X", T.X[:, 0:3072], T.xw[:])
+    D("s", "lm", "", "LM", T.LM[:], T.lm[:])
     D("s", "sd", "", "SD", T.SD[:], T.sd[:])
-    D("a", "xw", "", "X", T.X[:, 0:3072], T.xw[:])
-    D("a", "lm", "", "LM", T.LM[:], T.lm[:])
     D("s", "pk", "", "PK", T.PK[:], T.pk[:])
-    D("s", "rt", "", "RT", T.RT[:, 0:3], T.rt[:])
+    D("a", "rt", "", "RT", T.RT[:, 0:3], T.rt[:])
 
     def iota(nm, pattern, base=0, cm=0, exact=True):
         if exact:
@@ -139,379 +167,332 @@ def rank_program(g, core, T, topo):
         else:
             emit("g", lambda: g.iota(T[nm][:], pattern, base, cm, allow_small_or_imprecise_dtypes=True), [], [nm])
 
-    def select(nm, pattern, op, base, cm):
-        emit("g", lambda: g.affine_select(T[nm][:], T[nm][:], pattern, op, 0.0, base, cm), [nm], [nm])
+    def select(nm, src, pattern, op, x, base, cm):
+        emit("g", lambda: g.affine_select(T[nm][:], T[src][:], pattern, op, x, base, cm), [src], [nm])
     iota("PI", [[0, 16]], 0, 1)
-    iota("KI", [[1, 16]])
-    iota("ROWC", [[1, 128]], exact=False)
+    iota("ROWC", [[1, 144]], exact=False)
     iota("ROW8", [[16, 8]], exact=False)
-    iota("BIAS", [[0, 16], [-1, 16]], 15, exact=False)
-    iota("RST", [[0, 256]], 1, exact=False)
-    select("RST", [[0, 16], [1, 16]], OP.not_equal, 0, 0)
-    iota("CP", [[0, 256]], 1664, exact=False)
-    blocks = [[0, 16], [0, 8], [0, 16]]
-    iota("ONE", blocks, 1, exact=False)
-    select("ONE", [[-1, 16], [0, 8], [1, 16]], OP.is_equal, 0, 0)
-    select("ONE", [[0, 16], [-16, 8], [0, 16]], OP.is_ge, 0, 1)
-    select("ONE", [[0, 16], [16, 8], [0, 16]], OP.is_ge, 15, -1)
-    for nm, x in (("BLK", 1), ("NBLK", -1), ("BLKQ", 4096)):
-        iota(nm, [[0, 128]], x, exact=False)
-        select(nm, [[-16, 8], [0, 16]], OP.is_ge, 0, 1)
-        select(nm, [[16, 8], [0, 16]], OP.is_ge, 15, -1)
-    iota("LT", blocks, 4096, exact=False)
-    select("LT", [[0, 16], [-16, 8], [0, 16]], OP.is_ge, 0, 1)
-    select("LT", [[1, 16], [16, 8], [0, 16]], OP.is_ge, -1, -1)
-    iota("CQ", [[0, 256]], -2048, exact=False)
-    iota("C255", [[0, 256]], 255, exact=False)
-    iota("CM", [[1, 256]], 1408, exact=False)
-    fill("CN2", T.CN2[:], -1664.0)
-    fill("HB", T.HB[:], -0.5)
-    fill("EB", T.EB[:], -8.0)
-    fill("ONES", T.ONES[:], 1.0 / 128)
-    for i, x in enumerate((12288.0, 8192.0, 4096.0, -1664.0, BIG)):
+    iota("ROW16", [[0, 16], [1, 16]], exact=False)
+    iota("CM", [[1, 256]], 9600, exact=False)
+    fill("ZERO", T.ZERO[:], 0.0)
+    for nm, x in SCALED:
+        select(nm, "ZERO", [[-1, 128]], OP.not_equal, x, 0, 1)
+    for i, (_, x) in enumerate(BIASES):
         fill("BB", T.BB[:, i:i + 1], x)
-    cp("PI", "PF", T.PF[:], T.PI[:])
-    ts("ROWC PF", "ID", T.ID[:], T.ROWC[:], T.PF[:, 0:1], OP.is_equal)
-    ts("PI", "PQ", T.PQ[:], T.PI[:], 15, OP.bitwise_and)
-    tt("PQ KI", "KM", T.KM[:], T.PQ[:], T.KI[:], OP.is_equal)
-    for k in range(16):
-        ts("ID KM", "SEL", T.SEL[:, k, :], T.ID[:], T.KM[:, k:k + 1], OP.mult)
+    for nm, x in (("ONE", 1.0), ("NONE", -1.0), ("N1K", -1280.0), ("AVG", 1.0 / 128)):
+        fill(nm, T[nm][:], x)
+    cp("PI", "PF", T.PF[:, 0:1], T.PI[:, 0:1])
+    ts("PI", "PQ", T.PQ[:, 0:1], T.PI[:, 0:1], 15, OP.bitwise_and)
+    ts("PI", "PQ", T.PQ[:, 1:2], T.PI[:, 0:1], 112, OP.bitwise_and)
+    cp("PQ", "PF", T.PF[:, 1:3], T.PQ[:, 0:2])
+    ts("ROWC PF", "ID", T.ID[:], T.ROWC[:, 0:128], T.PF[:, 0:1], OP.is_equal)
+    ts("ROW8 PF", "GB", T.GB[:], T.ROW8[:], T.PF[:, 2:3], OP.is_equal)
+    ts("GB", "GS", T.GS[:], T.GB[:], 16.0, OP.mult)
+    ts("ROW16", "BIAS", T.BIAS[:], T.ROW16[:], -1.0, OP.mult, 15.0, OP.add)
+    ts("ROW16", "RST", T.RST[:], T.ROW16[:], 0.0, OP.is_gt)
 
-    def gather_tools(t):
+    def late_constants():
+        ts("ROWC PF", "SH", T.SH[:], T.ROWC[:], -15.0, OP.add, T.PF[:, 2:3], OP.is_equal)
+        ts("ROWC ROW16", "BLK", T.BLK[:], T.ROW16[:, 0:128], -1.0, OP.mult)
+        tt("ROWC BLK", "BLK", T.BLK[:], T.ROWC[:, 0:128], T.BLK[:], OP.add)
+        ts("BLK PF", "NBLK", T.NBLK[:], T.BLK[:], T.PF[:, 2:3], OP.is_equal, -1.0, OP.mult)
+        ts("BLK PF", "BLKQ", T.BLKQ[:], T.BLK[:], T.PF[:, 2:3], OP.is_equal, 4096.0, OP.mult)
+        ts("BLK PF", "BLK", T.BLK[:], T.BLK[:], T.PF[:, 2:3], OP.is_equal)
+        ts("ROW16 PF", "MASK", T.MASK[:], T.ROW16[:], T.PF[:, 1:2], OP.not_equal, 8192.0, OP.mult)
+        ts("ROW16 PF", "b7", at("b7l"), T.ROW16[:], T.PF[:, 1:2], OP.is_equal)
+        tt("CM b7", "b7", at("b7l"), T.CM[:], at("b7l"), OP.mult)
+        ts("b7", "CM", T.CM[:], at("b7l"), -4096.0, OP.add)
+        ts("RT", "RS", T.RS[:, 0:3], T.RT[:, 0:3], 8.0, OP.add)
+
+    def tools(t):
         J = "J%d" % (t % 2)
-        cp("TT " + J, "A16", T.A16[:], T.TT[:].indirect(T[J][:]))
+        ts("JT " + J, "A32", T.A32[:], T.JT[:].indirect(T[J][:]), 4095, OP.bitwise_and)
+        cp("A32", "A16", T.A16[:], T.A32[:])
 
-    def gather_jobs(t):
+    def nexts(t):
         J = "J%d" % (t % 2)
-        ac, nf = "AC%d" % (t % 2), "NF%d" % (t % 2)
-        if t == 0:
-            ts("JT", "NT", T.NT[:], T.JT[:], 12, OP.logical_shift_right)
-        cp("NT " + J, "N16", T.N16[:], T.NT[:].indirect(T[J][:]))
-        if t:
-            act("LM " + J, "LJ", T.LJ[:], T.LM[:].indirect(T[J][:]))
-        ts("A16", "TA", T.TA[:], T.A16[:], -1.0, OP.mult, 1408.0, OP.add)
-        ts("A16", ac, T[ac][:], T.A16[:], -1664.0, OP.add)
-        cp("N16", nf, T[nf][:], T.N16[:])
+        act("JT " + J, "NX", T.NX[:], T.JT[:].indirect(T[J][:]), bias="job", scale=1.0 / 4096)
 
-    defer, dd, held = [], [], []
+    def forms():
+        ts("NX", "N16", T.N16[:], T.NX[:], -1280.0, OP.add)
+        ts("A16", "AC", T.AC[:], T.A16[:], -1664.0, OP.add)
 
-    def flush_d():
-        while dd:
-            dd.pop(0)()
+    def limits(t):
+        J = "J%d" % (t % 2)
+        act("LM " + J, "LJ", T.LJ[:], T.LM[:].indirect(T[J][:]))
 
-    def flush():
-        if defer:
-            defer.pop(0)()
+    def gather(what, q, cs):
+        s, w = slice(32 * cs[0], 32 * cs[-1] + 32), slice(512 * cs[0], 512 * cs[-1] + 512)
+        W = " ".join("%s%d" % (what, c) for c in cs)
+        if what == "GN":
+            src = T.JT[:].indirect(T.N16[:, s])
+            if q == "a":
+                act("JT N16", W, T.GN[:, w], src, bias="job", scale=1.0 / 4096)
+            else:
+                ts("JT N16", W, T.GN[:, w], src, 1.0 / 4096, OP.mult, 1279.625, OP.add)
+        else:
+            tab = "X" if what == "XG" else "SD"
+            (act if q == "a" else cp)(tab + " A16", W, T[what][:, w], T[tab][:, 0:3072].indirect(T.A16[:, s]))
 
-    def gather_d(c):
-        w = slice(1024 * c, 1024 * c + 1024)
-        s = slice(64 * c, 64 * c + 64)
-        act("SD A16", "GD%d" % c, T.GD[:, w], T.SD[:].indirect(T.A16[:, s]))
+    def diagonal(place, what, h, first=None, stop=True):
+        if first:
+            mm(first[0] + " " + first[1], place[:2], at(place, 128 * h, 128 * h + 128), T[first[0]][:, 128 * h:128 * h + 128], T[first[1]][:], True, False)
+        pick(place, what, h, "ID", lambda k: T.ID[:, k::16], stop)
 
-        def later():
-            for k in range(16):
-                mm("GD%d SEL" % c, "b3", T.b3[:, s], T.SEL[:, k, :], T.GD[:, w.start + k:w.stop:16], k == 0, False)
-            mm("ID CN2", "b3", T.b3[:, s], T.ID[:], T.CN2[:, s], False, True)
-        dd.append(later)
+    def sisters(h):
+        diagonal("b0l", "GD", h, ("AC", "ID"))
 
-    def gather_n(c, t):
-        nf = "NF%d" % (t % 2)
-        w = slice(1024 * c, 1024 * c + 1024)
-        s = slice(64 * c, 64 * c + 64)
-        cp("NT N16", "GN%d" % c, T.GN[:, w], T.NT[:].indirect(T.N16[:, s]))
+    def wraps():
+        act("b0", "WR", T.WR[:], at("b0l"), AF.Sign, bias="wrap")
+        add("b0h", [("IW", "WR")], start=True)
+        for h in range(2):
+            diagonal("b0h", "GD", h, None, h == 1)
 
-        def later():
-            o = T.b3[:, 256 + 64 * c:320 + 64 * c]
-            for k in range(16):
-                mm("GN%d SEL" % c, "b3", o, T.SEL[:, k, :], T.GN[:, w.start + k:w.stop:16], k == 0, False)
-            mm("NID " + nf, "b3", o, T.NID[:], T[nf][:, s], False, True)
-        defer.append(later)
+    def seconds(h):
+        diagonal("b1l", "GN", h, ("NX", "NID"))
 
     def sums(h):
-        for k in range(16):
-            mm("XG%d XG%d IB" % (2 * h, 2 * h + 1), "b4", T.b4[:, 128 * h + k:128 * h + 128:16], T.XG[:, 2048 * h + k:2048 * h + 2048:16],
-               T.IB[:], False, h == 1 and k == 15)
+        if h == 0:
+            add("b3l", [("ID", "LJ")], True, True)
+            add("b3h", [("AVG", "BIAS")], True)
+        pick("b3h", "XG", h, "GS", lambda k: T.GS[:], h == 1)
 
     def heavy():
-        V("RST b4", "PM", lambda: g.vector.tensor_tensor_scan(out=T.PM[:], data0=T.RST[:], data1=lo(T.b4), initial=0.0, op0=OP.mult, op1=OP.max))
-        cp("PM", "PM", T.PM[:, 7::16], T.PM[:, 15::16])
-        cp("PM", "PM", T.PM[:, 3::8], T.PM[:, 7::8])
-        cp("PM", "PM", T.PM[:, 1::4], T.PM[:, 3::4])
-        cp("PM", "PM", T.PM[:, 0::2], T.PM[:, 1::2])
-        tt("b4 PM", "HT", T.HT[:], lo(T.b4), T.PM[:], OP.is_equal)
+        scan("RST b3", "PM", T.PM[:], T.RST[:], at("b3h"), 0.0, OP.mult, OP.max)
+        scan("RST PM", "PX", T.PX[:, ::-1], T.RST[:], T.PM[:, ::-1], 0.0, OP.mult, OP.max)
+        tt("PX b3", "HT", T.HT[:], T.PX[:], at("b3h"), OP.is_equal)
         for h in range(2):
-            mm("HT ID", "b5", T.b5[:, 128 * h:128 * h + 128], T.HT[:, 128 * h:128 * h + 128], T.ID[:], True, True)
-        act("b5", "H", T.H[:], lo(T.b5))
+            mm("HT ID", "b4", T.b4[:, 128 * h:128 * h + 128], T.HT[:, 128 * h:128 * h + 128], T.ID[:], True, True)
 
-    def over_a(i):
-        b = "b%d" % (i % 2)
-        for k, o in ((2 * i, lo(T[b])), (2 * i + 1, hi(T[b]))):
-            mm("NID LJ", b, o, T.NID[:], T.LJ[:], True, False)
-            mm("XG0 XG1 XG2 XG3 ID", b, o, T.ID[:], T.XG[:, k::16], False, True)
-        act(b + " HB", "OVA%d" % i, T.OV[:, 512 * i:512 * i + 512], T[b][:], AF.Sign, bias=T.HB[:])
+    def heavy_a():
+        act("b4", "H", T.H[:], at("b4l"))
 
-    def count_a(i, end):
-        for k in (2 * i, 2 * i + 1):
-            mm("OVA%d ONE" % i, "b2", lo(T.b2), T.ONE[:, k, :], T.OV[:, 256 * k:256 * k + 256], k == 0, k == end)
-
-    def wear(t, fillers):
-        kd = KDS[t]
-        for c in range(4):
-            if c not in XV[t]:
-                act("X A16", "XG%d" % c, T.XG[:, 1024 * c:1024 * c + 1024], T.X[:, 0:3072].indirect(T.A16[:, 64 * c:64 * c + 64]))
-        fillers(0)
-        mm("ONES BIAS", "b4", lo(T.b4), T.ONES[:], T.BIAS[:], True, False)
-        for c in XV[t]:
-            cp("X A16", "XG%d" % c, T.XG[:, 1024 * c:1024 * c + 1024], T.X[:, 0:3072].indirect(T.A16[:, 64 * c:64 * c + 64]))
-        sums(0)
-        sums(1)
-        mm("ID LJ", "b7", lo(T.b7), T.ID[:], T.LJ[:], True, True)
-        for i in range(kd // 2):
-            over_a(i)
-            if i:
-                count_a(i - 1, 15)
-            if i == 3:
-                heavy()
-                fillers(1)
-            if i in FL:
-                flush()
-        count_a(kd // 2 - 1, 15)
-        while defer:
-            flush()
-        for k in range(kd, 16):
-            tt("XG0 XG1 XG2 XG3 b7", "OVD%d" % k, T.OV[:, 256 * k:256 * k + 256], T.XG[:, k::16], lo(T.b7), OP.is_gt)
-        for k in range(kd, 16):
-            mm("OVD%d ONE" % k, "b2", lo(T.b2), T.ONE[:, k, :], T.OV[:, 256 * k:256 * k + 256], False, k == 15)
-        fillers(2)
-
-    def list_of(R, src, o):
-        for r in range(16):
-            mm(R + " ONE", "b7", T.b7[:, o:o + 16], T.ONE[:, r, :], src[:, r::16], r == 0, r == 15)
+    def compare(ks):
+        for k in ks:
+            tt(" ".join("XG%d" % c for c in range(8)) + " b3", "OV%d" % k, part("OV", k), T.XG[:, k::16], at("b3l"), OP.is_gt)
+            for h in range(2):
+                mm("OV%d GB" % k, "b2", T.b2[:, 128 * h + k:128 * h + 128:16], T.OV[:, 256 * k + 128 * h:256 * k + 128 * h + 128], T.GB[:], True, True)
 
     def pocket3(t):
-        return ("Q3", T.Q[:, 768:1024]) if t == 0 else ("LAND%d" % t, T["LAND%d" % t][:])
+        return ("Q3", part("Q", 3)) if t == 0 else ("LAND%d" % t, T["LAND%d" % t][:])
+
+    def init_pockets_a():
+        act("PK", "FH", T.FH[:], T.PK[:], bias="job", scale=1.0 / 4096)
+        for i, (place, bits) in enumerate((("b6l", "IF"), ("b6h", "I8"), ("b7l", "I4"), ("b7h", None))):
+            add(place, [("IF", ("FH", part("FH", i))), ("IF", "N1K")] + ([(bits, "ONE")] if bits else []), True, True)
+
+    def init_pockets():
+        ts("PK", "M0 M1 M2 M3", T.M[:], T.PK[:], 4095, OP.bitwise_and)
+        for b, s in (("b6", slice(0, 512)), ("b7", slice(512, 1024))):
+            tt("PK " + b, "Q0 Q1" if b == "b6" else "Q2 Q3", T.Q[:, s], T.PK[:, s], T[b][:], OP.add)
 
     def victims(t):
         q3, l3 = pocket3(t)
-        tt("Q0 Q1", "b5", hi(T.b5), T.Q[:, 0:256], T.Q[:, 256:512], OP.max)
-        tt("b5 Q2", "b5", hi(T.b5), T.Q[:, 512:768], hi(T.b5), OP.max)
-        tt("b5 " + q3, "EV", T.EV[:], l3, hi(T.b5), OP.max)
+        tt("Q0 Q1", "b2", at("b2h"), part("Q", 0), part("Q", 1), OP.max)
+        tt("Q2 b2", "b2", at("b2h"), part("Q", 2), at("b2h"), OP.max)
+        tt(q3 + " b2", "EV", T.EV[:], l3, at("b2h"), OP.max)
+        if t:
+            ts(q3, "M3", part("M", 3), l3, 4095, OP.bitwise_and)
         ts("EV", "ME", T.ME[:], T.EV[:], 4095, OP.bitwise_and)
         ts("EV", "IX", T.IX[:], T.EV[:], 12, OP.logical_shift_right, 3, OP.bitwise_and)
-        for i in range(3):
-            ts("IX", "GI%d" % i, T.GI[:, 256 * i:256 * i + 256], T.IX[:], float(3 - i), OP.is_equal)
-        ts("ME", "MC", T.MC[:], T.ME[:], -1664.0, OP.add)
-        if t:
-            ts(q3, "M3", T.M[:, 768:1024], l3, 4095, OP.bitwise_and)
 
-    def init_pockets():
-        ts("PK", "SH", T.SH[:], T.PK[:], 12, OP.logical_shift_right)
-        ts("PK", "M0 M1 M2 M3", T.M[:], T.PK[:], 4095, OP.bitwise_and)
-        for i in range(4):
-            s = slice(256 * i, 256 * i + 256)
-            ts("SH", "b6", hi(T.b6), T.SH[:, s], 12288.0, OP.mult, 4096.0 * (3 - i), OP.add)
-            tt("PK b6", "Q%d" % i, T.Q[:, s], T.PK[:, s], hi(T.b6), OP.add)
+    def victims_a():
+        act("ME", "MC", T.MC[:], T.ME[:], bias="name")
+        act("IX", "IXB", T.IXB[:], T.IX[:])
+        act("IX", "B1", T.B1[:], T.IX[:], AF.Sign, bias="bit")
 
-    def finish_pockets():
-        ts("Q0 Q1 Q2", "SH", T.SH[:, 0:768], T.Q[:, 0:768], 14, OP.logical_shift_right)
-        for i in range(3):
-            s = slice(256 * i, 256 * i + 256)
-            b = ("b0", "b1", "b2")[i]
-            ts("SH", b, lo(T[b]), T.SH[:, s], -12288.0, OP.mult, -4096.0 * (3 - i), OP.add)
-            tt("Q%d " % i + b, "OUTP%d" % i, T.OUTP[:, s], T.Q[:, s], lo(T[b]), OP.add)
-        D("s", "oq", "OUTP0 OUTP1 OUTP2", "YP", T.yp[:, 0:768], T.OUTP[:])
+    banks = ("b0", "b1", "b5")
 
-    def sel(i, t):
-        s = slice(256 * i, 256 * i + 256)
-        eq = [T.EQ[:, 256 * j:256 * j + 256] for j in range(4)]
-        b, o = (("b6", lo(T.b6)), ("b6", hi(T.b6)), ("b4", lo(T.b4)))[i]
-        mm("ID8 EQ%d" % i, b, o, T.ID8[:], eq[i], True, False)
-        for j in range(4):
-            if j < i:
-                mm("NID16 EQ%d" % j, b, o, T.NID16[:], eq[j], False, False)
-            elif j > i:
-                mm("NID EQ%d" % j, b, o, T.NID[:], eq[j], False, False)
-        mm("ID GI%d" % i, b, o, T.ID[:], T.GI[:, s], False, True)
-        if t == 2:
-            act(b, b, o, o, AF.Relu)
-            act(b, "SL%d" % i, T.SL[:, s], o, AF.Sign)
+    def eq(i):
+        return ("EQ%d" % i, part("EQ", i))
+
+    def chosen(i):
+        terms = [(("ID", "NID", "ID")[i], "IXB")] + ([(("IK", "IW")[i - 1], "B1")] if i else [])
+        terms += [("I4" if j == i else "NID", eq(j)) for j in range(i, 4)] + [("NB", eq(j)) for j in range(i)]
+        add(banks[i] + "l", terms, True, True)
+        act(banks[i], "SG%d" % i, part("SG", i), at(banks[i] + "l"), AF.Sign, bias="s%d" % i)
+
+    def masks(i, last):
+        sg = ("SG%d" % i, part("SG", i))
+        if last:
+            add(banks[i] + "l", [("NF", ("FH", part("FH", i))), ("NB", sg), ("IM", "NONE"), (("IF", "I8", "I4")[i], "NONE")], True, True)
+            add(banks[i] + "h", [("I4", "NN"), ("IL", sg), ("IC", sg), ("ID", "UC")], True, True)
         else:
-            held.append(lambda: ts(b, "SL%d" % i, T.SL[:, s], o, 0.5, OP.is_ge))
+            add(banks[i] + "l", [("NB", sg)], True, True)
+            add(banks[i] + "h", [("IQ", "NN"), ("IB", sg), ("IP%d" % i, sg), ("ID", "UC")], True, True)
 
-    def update(t):
-        at = (("b0", lo(T.b0)), ("b0", hi(T.b0)), ("b1", lo(T.b1)))
-        for i, (b, o) in enumerate(at):
-            tt("Q%d " % i + b, b, o, o, T.Q[:, 256 * i:256 * i + 256], OP.subtract)
-        for i, (b, o) in enumerate(at):
-            s = slice(256 * i, 256 * i + 256)
-            if held:
-                held.pop(0)()
-            tt("SL%d " % i + b, b, o, T.SL[:, s], o, OP.mult)
-            tt("Q%d " % i + b, "Q%d" % i, T.Q[:, s], T.Q[:, s], o, OP.add)
-            if t < 2:
-                ts("Q%d" % i, "M%d" % i, T.M[:, s], T.Q[:, s], 4095, OP.bitwise_and)
+    def update(last):
+        new = "OUTP" if last else "Q"
+        for i, b in enumerate(banks):
+            tt("Q%d " % i + b, "TQ%d" % i, part("TQ", i), part("Q", i), at(b + "l"), OP.add if last else OP.min)
+        for i, b in enumerate(banks):
+            tt("TQ%d " % i + b, new + str(i), part(new, i), part("TQ", i), at(b + "h"), OP.max)
+        if not last:
+            ts("Q0 Q1 Q2", "M0 M1 M2", T.M[:, 0:768], T.Q[:, 0:768], 4095, OP.bitwise_and)
 
-    def wrap():
-        tt("TA b3", "b4", hi(T.b4), T.TA[:], lo(T.b3), OP.is_gt)
+    def give_mask(t):
+        add("b0h", ([("NF", "FE"), ("NF", "N1K")] if t == 2 else []) + [("N4", "IXB")] + [("NB", eq(j)) for j in range(4)], True, True)
+
+    def give_pocket(t):
+        q3, l3 = ("Q3F", T.Q3F[:]) if t == 2 else pocket3(t)
+        t2 = "T2F" if t == 2 else "T2%d" % t
+        tt(q3 + " b2", t2, T[t2][:], l3, at("b2h"), OP.min)
+
+    def give(t):
+        t1, t2 = ("T1F", "T2F") if t == 2 else ("T1%d" % t, "T2%d" % t)
+        tt("EV b0", t1, T[t1][:], T.EV[:], at("b0h"), OP.add)
+        rid, pid = topo.addr(nxt)[0:2]
+        send = RemoteDMATransfer(dst_ids=[DstId(rid=rid, pnc=pid)], dma_engine_mask=topo.mask(core, nxt), remote_sem=T.sem["ar%d" % t],
+                                 srcs=[T[t1][:], T[t2][:]], dsts=[T["LAND%d" % (t + 1)][:]], alu_op=2)
+        emit("g", lambda: g.remote_dma_fused([send], local_sem=T.sem["lc%d" % t]), [t1, t2], [], "lc%d" % t, 0, len(topo.engines(core, nxt)))
+        wrote["LAND%d" % (t + 1)] = ("ar%d" % t, len(topo.engines(prv, core)))
+
+    def plain_forms():
+        act("EV", "FE", T.FE[:], T.EV[:], bias="key", scale=1.0 / 16384)
+        act("LAND2", "F3", T.F3[:], T.LAND2[:], bias="key", scale=1.0 / 16384)
+        act("Q0 Q1 Q2", "FH", T.FH[:, 0:768], T.Q[:, 0:768], bias="key", scale=1.0 / 16384)
+        add("b6l", [("NF", "F3"), ("NF", "N1K")], True, True)
+        tt("LAND2 b6", "Q3F", T.Q3F[:], T.LAND2[:], at("b6l"), OP.add)
 
     cp("JM", "J0", T.J0[:], T.JM[:])
-    ts("JT", "TT", T.TT[:], T.JT[:], 4095, OP.bitwise_and)
-    gather_tools(0)
-    gather_jobs(0)
-    act("ID", "NID", T.NID[:], T.ID[:], scale=-1.0)
-    for c in range(4):
-        gather_d(c)
-        flush_d()
-    act("LM J0", "LJ", T.LJ[:], T.LM[:].indirect(T.J0[:]))
-    for nm, f in (("ID8", 8.0), ("NID16", -16.0), ("IDQ", 16384.0), ("IDM", -1408.0), ("IDW", 3072.0)):
-        act("ID", nm, T[nm][:], T.ID[:], scale=f)
-
-    def first(x):
-        if x == 0:
-            for c in range(4):
-                gather_n(c, 0)
-            wrap()
-            ts("PI", "PG", T.PG[:], T.PI[:], 112, OP.bitwise_and)
-            tt("PG KI", "CK", T.CK[:], T.PG[:], T.KI[:], OP.add)
-            ts("ROW8 CK", "IB", T.IB[:], T.ROW8[:], T.CK[:, 0:1], OP.is_equal, 16.0, OP.mult)
-            ts("RT", "RTF", T.RTF[:, 0:3], T.RT[:, 0:3], -1.0, OP.mult, 255.0, OP.add)
-            for t in range(3):
-                ts("PQ", "THR", T.THR[:, t:t + 1], T.PQ[:, 0:1], KDS[t] - 0.5, OP.is_ge, 8.0, OP.mult)
-        elif x == 1:
-            init_pockets()
-        else:
-            victims(0)
-    wear(0, first)
+    nexts(0)
+    tools(0)
+    forms()
+    gather("GN", "a", (0, 1))
+    gather("GN", "v", (2, 3))
+    gather("GN", "a", (4, 5))
+    late_constants()
+    limits(0)
+    gather("XG", "v", (0, 1))
+    gather("XG", "a", (4, 5))
+    gather("XG", "v", (2, 3))
+    gather("XG", "a", (6, 7))
+    seconds(0)
+    sums(0)
+    sums(1)
+    for c in (0, 2, 4):
+        gather("GD", "a", (c, c + 1))
+    heavy()
+    compare(range(8))
+    init_pockets_a()
+    gather("GD", "a", (6, 7))
+    sisters(0)
+    compare(range(8, 16))
+    sisters(1)
+    heavy_a()
+    wraps()
+    init_pockets()
+    victims(0)
+    victims_a()
 
     for t in range(3):
         last = t == 2
         J, J2 = "J%d" % (t % 2), "J%d" % ((t + 1) % 2)
-        ac, nf = "AC%d" % (t % 2), "NF%d" % (t % 2)
-
-        def tool(b, o, first, stop):
-            mm("ID " + ac, b, o, T.ID[:], T[ac][:], first, False)
-            mm("ID CP", b, o, T.ID[:], T.CP[:], False, False)
-            mm("IDM COND", b, o, T.IDM[:], T.COND[:], False, False)
-            mm("ID CD", b, o, T.ID[:], T.CD[:], False, False)
-            mm("IDW CW", b, o, T.IDW[:], T.CW[:], False, stop)
-        ts("b2 THR", "COND", T.COND[:], lo(T.b2), T.THR[:, t:t + 1], OP.is_gt)
-        tt("COND b3", "CN", T.CN[:], T.COND[:], hi(T.b3), OP.mult)
-        mm("ID " + nf, "b6", hi(T.b6), T.ID[:], T[nf][:], True, False)
-        mm("ID CN", "b6", hi(T.b6), T.ID[:], T.CN[:], False, True)
-        act("b6", "NN", T.NN[:], hi(T.b6))
-        tt("COND b3", "CD", T.CD[:], T.COND[:], lo(T.b3), OP.mult)
-        tt("COND b4", "CW", T.CW[:], T.COND[:], hi(T.b4), OP.mult)
-        tool("b6", lo(T.b6), True, True)
-        if not last:
-            tt("NN b5", "NH", T.NH[:], T.NN[:], lo(T.b5), OP.mult)
-        tt("MC b5", "G1", T.G1[:], T.MC[:], lo(T.b5), OP.mult)
+        add("b0l", [("ID", "AC"), ("IC", "ONE")], start=True)
+        add("b5l", [("ID", "MC")], True, True)
+        add("b3l", [("ID", "AC")], start=True)
+        add("b7l", [("ID", "MASK")], start=True)
+        ts("b2", "COND", T.COND[:], at("b2l"), 8.5, OP.is_gt)
+        tt("COND b0", "CU", T.CU[:], T.COND[:], at("b0h"), OP.mult)
+        add("b3l", [("~IW", "COND")])
+        add("b0l", [("~IW", "COND"), ("~ID", "CU")], stop=True)
+        add("b3l", [("~ID", "CU")], stop=True)
+        tt("H b5", "G1", T.G1[:], T.H[:], at("b5l"), OP.mult)
+        add("b7l", [("BLK", "G1")])
+        add("b6l", [("BLK", "G1")], start=True)
+        for cs in B1[t]:
+            gather("GN", "a", cs)
+        if t:
+            seconds(0)
         for i in range(4):
-            tt("M%d b6" % i, "EQ%d" % i, T.EQ[:, 256 * i:256 * i + 256], T.M[:, 256 * i:256 * i + 256], lo(T.b6), OP.is_equal)
-        act("b6 BB", "UC", T.UC[:], lo(T.b6), AF.Identity, bias=T.BB[:, 3:4])
+            tt("M%d b0" % i, "EQ%d" % i, part("EQ", i), part("M", i), at("b0l"), OP.is_equal)
+            add("b2h", [("IB", eq(i))], i == 0, i == 3)
+        give_mask(t)
+        tt("H b2", "HH", T.HH[:], T.H[:], at("b2h"), OP.min)
+        give_pocket(t)
+        tt("HH b3", "G2", T.G2[:], T.HH[:], at("b3l"), OP.mult)
+        tt("HH b5", "G3", T.G3[:], T.HH[:], at("b5l"), OP.mult)
+        add("b7l", [("BLK", "G2")])
+        add("b6l", [("BLK", "G2"), ("NBLK", "G3")], stop=True)
+        add("b7l", [("NBLK", "G3")], stop=True)
+        add("b4l", [("BLK", "HH")], True, True)
+        seconds(1)
+        add("b1h", [("ID", "NX")], start=True)
+        give(t)
+        act("b6", "VR", T.VR[:], at("b6l"))
+        scan("CM b7", "PV", T.PV[:], T.CM[:], at("b7l"), -4096.0, OP.max, OP.min)
+        act("b4 RS", "DL", T.DL[:], at("b4l"), bias="rest", scale=T.RS[:, t:t + 1])
+        act("b3", "UC", T.UC[:], at("b3l"))
         if not last:
-            act("b6", "UU", T.UU[:], lo(T.b6))
-            list_of("NH", T.NH, 288)
-        for i in range(4):
-            mm("ID EQ%d" % i, "b2", hi(T.b2), T.ID[:], T.EQ[:, 256 * i:256 * i + 256], i == 0, i == 3)
+            add("b4h", [("ID", "NX"), ("~IK", "HT")], start=True)
+        tt("COND b1", "CN", T.CN[:], T.COND[:], at("b1l"), OP.mult)
+        tt("PV b6", "E15", part("E", 15), T.PV[:], at("b6l"), OP.is_equal)
+        add("b1h", [("~ID", "CN")], stop=True)
+        act("b1", "NN", T.NN[:], at("b1h"), bias="next")
         if not last:
-            cp("b7", J2, T[J2][:], T.b7[:, 288:304])
-        tt("H b2", "b5", hi(T.b5), T.H[:], hi(T.b2), OP.min)
-        tt("MC b5", "G3", T.G3[:], T.MC[:], hi(T.b5), OP.mult)
-        tt("UC b5", "G2", T.G2[:], T.UC[:], hi(T.b5), OP.mult)
-        act("b5", "HH", T.HH[:], hi(T.b5))
-        act("b2 BB", "b2", lo(T.b2), hi(T.b2), AF.Relu, scale=-BIG, bias=T.BB[:, 4:5])
-        mm("BLK G1", "b7", lo(T.b7), T.BLK[:], T.G1[:], True, False)
-        mm("NBLK G3", "b7", lo(T.b7), T.NBLK[:], T.G3[:], False, False)
-        mm("BLK G2", "b7", lo(T.b7), T.BLK[:], T.G2[:], False, True)
-        mm("BLK HH", "b2", hi(T.b2), T.BLK[:], T.HH[:], True, True)
+            add("b4h", [("~ID", "CN")], stop=True)
+            act("b4", "NH", T.NH[:], at("b4h"), AF.Relu, bias="next")
+        add("b7h", [("ID", "MASK"), ("ID", "VR"), ("BLKQ", ("E15", part("E", 15)))], start=True)
         if not last:
-            cp("UU " + J, "TT", T.TT[:].indirect(T[J][:]), T.UU[:])
-        cp("b7", "VR", T.VR[:], lo(T.b7))
-        list_of("VR", T.VR, 256)
-        act("b2", "UP", T.UP[:], hi(T.b2))
-
-        def give():
-            q3, l3 = pocket3(t)
-            tt(q3 + " b2", "b2", lo(T.b2), l3, lo(T.b2), OP.max)
-            tt("EV b2", "S1", T.S1[:], T.EV[:], lo(T.b2), OP.min)
-            sb = "SB%d" % t
-            if not last:
-                ts("S1", sb, T[sb][:], T.S1[:], 0xFFCFFF, OP.bitwise_and)
-            else:
-                ts("S1", "IX", T.IX[:], T.S1[:], 14, OP.logical_shift_right)
-                ts("S1", "S2", T.S2[:], T.S1[:], 0xFFCFFF, OP.bitwise_and)
-                ts("IX", "b2", lo(T.b2), T.IX[:], -12288.0, OP.mult)
-                tt("S2 b2", sb, T[sb][:], T.S2[:], lo(T.b2), OP.add)
-            rid, pid = topo.addr(nxt)[0:2]
-            emit("g", lambda: g.remote_dma(out_ap=T["LAND%d" % (t + 1)][:], in_ap=T[sb][:], remote_sem=T.sem["ar%d" % t], local_sem=T.sem["lc%d" % t],
-                                           pid=pid, routing_id=rid, dma_engine_mask=topo.mask(core, nxt)),
-                 [sb], [], "lc%d" % t, 0, len(topo.engines(core, nxt)))
-            wrote["LAND%d" % (t + 1)] = ("ar%d" % t, len(topo.engines(prv, core)))
-        if not last:
-            gather_tools(t + 1)
-            gather_d(0)
-            cp("NN " + J, "NT", T.NT[:].indirect(T[J][:]), T.NN[:])
-        else:
-            give()
-        ts("b7", "VL", T.VL[:], T.b7[:, 256:272], 0.0625, OP.mult, 1664.0, OP.add)
-        ts("b7", "VLF", T.VLF[:], T.b7[:, 256:272], 0.0625, OP.mult)
-        for q in range(16):
-            ts("VR VLF", "E%d" % q, T.E[:, 256 * q + 16 * q:256 * q + 256], T.VR[:, 16 * q:256], T.VLF[:, q:q + 1], OP.is_equal)
-        act("X VL EB", "Y2", T.Y2[:], T.X[:, 0:3072].indirect(T.VL[:]), AF.Relu, bias=T.EB[:])
-        act("X VL RTF", "Y1", T.Y1[:], T.X[:, 0:3072].indirect(T.VL[:]), AF.Relu, scale=-1.0, bias=T.RTF[:, t:t + 1])
-        mm("IDQ " + nf, "b1", hi(T.b1), T.IDQ[:], T[nf][:], True, False)
-        mm("IDQ CN", "b1", hi(T.b1), T.IDQ[:], T.CN[:], False, False)
-        tool("b1", hi(T.b1), False, True)
-        mm("ID CQ", "b5", lo(T.b5), T.ID[:], T.CQ[:], True, False)
+            add("b6h", [("I4", "NN"), ("ID", "UC")], True, True)
+            act("b6", "REC", T.REC[:], at("b6h"), bias="rec")
+            for r in range(16):
+                mm("NH SH", "b4", T.b4[:, 0:16], T.SH[:, 15 - r:143 - r], T.NH[:, r::16], r == 0, r == 15)
+            act("b4", J2, T[J2][:], T.b4[:, 0:16])
+        act("PV", "VL", T.VL[:], T.PV[:, 15::16], bias="list")
         for q in range(15):
-            mm("BLKQ E%d" % q, "b5", T.b5[:, 16 * q + 16:256], T.BLKQ[:], T.E[:, 256 * q + 16 * q + 16:256 * q + 256], False, False)
-        ee = " ".join("E%d" % q for q in range(16))
-        for r in range(1, 16):
-            mm("LT " + ee, "b5", T.b5[:, r:256:16], T.LT[:, r, :], T.E[:, r::272], False, r == 15)
+            ts("VR PV", "E%d" % q, T.E[:, 256 * q + 16 * q + 16:256 * q + 256], T.VR[:, 16 * q + 16:256], T.PV[:, 16 * q + 15:16 * q + 16], OP.is_equal)
+            mm("BLKQ E%d" % q, "b7", T.b7[:, 256 + 16 * q + 16:512], T.BLKQ[:], T.E[:, 256 * q + 16 * q + 16:256 * q + 256], False, q == 14)
         if not last:
-            give()
-        tt("CM b5", "YM", T.YM[:], T.CM[:], lo(T.b5), OP.min)
-        tt("YM b7", "OF", T.OF[:], T.YM[:], lo(T.b7), OP.max)
-        mm("ID C255", "b5", hi(T.b5), T.ID[:], T.C255[:], True, False)
-        mm("NID Y1", "b5", hi(T.b5), T.NID[:], T.Y1[:], False, False)
-        mm("NID Y2", "b5", hi(T.b5), T.NID[:], T.Y2[:], False, True)
-        list_of("OF", T.OF, 272)
+            limits(t + 1)
+            cp("REC " + J, "JT", T.JT[:].indirect(T[J][:]), T.REC[:])
+        chosen(0)
+        chosen(1)
+        scan("CM b7", "PO", T.PO[:], T.CM[:], at("b7h"), -4096.0, OP.max, OP.min)
         if not last:
-            gather_jobs(t + 1)
-        tt("UP b5", "YT", T.YT[:], T.UP[:], hi(T.b5), OP.mult)
+            tools(t + 1)
+            nexts(t + 1)
+        chosen(2)
+        tt("X VL DL", "Y1", T.Y1[:], T.X[:, 0:3072].indirect(T.VL[:]), T.DL[:], OP.add)
+        ts("PO", "OL", T.OL[:], T.PO[:, 15::16], -2432.0, OP.add)
+        ts("Y1", "Y2", T.Y2[:], T.Y1[:], 0.0, OP.max, 255.0, OP.min)
         if not last:
-            gather_d(1)
-        for i in range(3):
-            b, o = (("b0", lo(T.b0)), ("b0", hi(T.b0)), ("b1", lo(T.b1)))[i]
-            act("b1 BB", b, o, hi(T.b1), AF.Identity, bias=T.BB[:, i:i + 1])
-        ts("b7", "OL", T.OL[:], T.b7[:, 272:288], 0.0625, OP.mult, 1664.0, OP.add)
-        V("Y2 YT OL", "X", lambda: g.vector.tensor_tensor(out=T.X[:].indirect(T.OL[:]), in0=T.Y2[:], in1=T.YT[:], op=OP.add))
+            for cs in B2:
+                gather("GD", "a", cs)
+            forms()
+        cp("Y2 OL", "X", T.X[:].indirect(T.OL[:]), T.Y2[:])
         if last:
             D("s", "ox", "X", "YX", T.yx[:, 0:3072], T.X[:, 0:3072])
-            for i in range(3):
-                sel(i, t)
-            update(t)
-            finish_pockets()
+        for i in range(3):
+            masks(i, last)
+        if last:
+            update(last)
+            D("s", "oq", "OUTP0 OUTP1 OUTP2", "YP", T.yp[:, 0:768], T.OUTP[:])
             D("a", "o3", "LAND3", "YP3", T.yp[:, 768:1024], T.LAND3[:])
-        else:
-            gather_d(2)
-            gather_d(3)
-
-            def fillers(x):
-                if x == 0:
-                    for i in range(3):
-                        sel(i, t)
-                    flush_d()
-                    update(t)
-                    wrap()
-                    for c in range(NB):
-                        gather_n(c, t + 1)
-                elif x == 1:
-                    for c in range(NB, 4):
-                        gather_n(c, t + 1)
-                else:
-                    victims(t + 1)
-            wear(t + 1, fillers)
+            break
+        for c in (0, 2, 4, 6):
+            gather("XG", "a", (c, c + 1))
+        for what, cs in AV:
+            gather(what, "v", cs)
+        update(last)
+        sums(0)
+        victims(t + 1)
+        sums(1)
+        for cs in A1:
+            gather("GD", "a", cs)
+        heavy()
+        compare(range(6))
+        sisters(0)
+        victims_a()
+        heavy_a()
+        compare(range(6, 11))
+        sisters(1)
+        wraps()
+        for cs in A2:
+            gather("GN", "a", cs)
+        compare(range(11, 16))
+        if t == 1:
+            plain_forms()
     for s in ("sv", "sa", "st", "sg"):
         g.wait_ge(T.sem[s], count[s])
     for d in DMAS:

@@ -4,13 +4,18 @@ from concourse.mybir import AluOpType, ActivationFunctionType
 OP = AluOpType
 AF = ActivationFunctionType
 BIG = 16777216.0
-B2, A1, A2 = ((0, 1),), ((4, 5), (6, 7)), ((0, 1), (2, 3))
-B1 = (((6, 7),), ((4, 5), (6, 7)), ((4, 5), (6, 7)))
-AV = (("GD", (2, 3)),)
-SCALED = (("NID", -1.0), ("IW", -1536.0), ("IC", 1664.0), ("IK", 1024.0), ("IF", 12288.0), ("I8", 8192.0), ("I4", 4096.0), ("IB", BIG),
-          ("N4", -4096.0), ("NB", -BIG), ("IQ", 16384.0), ("IP0", 13952.0), ("IP1", 9856.0), ("IP2", 5760.0), ("NF", -12288.0), ("IL", 4194304.0), ("IM", 1048576.0))
-BIASES = (("job", 1279.625), ("key", 1279.53125), ("wrap", -1407.5), ("name", -1664.0), ("next", -2304.0), ("rec", 4195968.0), ("list", 1664.0),
-          ("rest", -8.0), ("bit", -1.5), ("s0", -2.5), ("s1", -1021.5), ("s2", -1536.5))
+CYCLE, TENSOR, GATHER, SCATTER, CALL, WAKE = 0.83, 0.42, 1.2, 3.2, 45.0, 60.0
+SLACK = 300.0
+ROUNDS = 4
+PIECE = 2
+VX = ((0, 1, 2, 3), (6, 7), (6, 7))
+VN = ((0, 1), (), ())
+VD = ((), (), ())
+SCALED = (("NID", -1.0), ("IF", 12288.0), ("I8", 8192.0), ("I4", 4096.0), ("IW", -1536.0), ("IC", 1664.0), ("IB", BIG), ("IK", 1024.0),
+          ("N4", -4096.0), ("NB", -BIG), ("I5", 5.0), ("N2", -2.0), ("IQ", 16384.0), ("IP0", 13952.0), ("IP1", 9856.0), ("IP2", 5760.0),
+          ("NF", -12288.0), ("IL", 4194304.0), ("IM", 1048576.0))
+JOB, KEY = 1279.625, 1279.53125
+BIASES = (JOB, KEY, -1280.0, -1407.5, -1664.0, -2304.0, 4195968.0, 1664.0, -8.0, -1.5, -2.5, -2432.0)
 
 
 def _s(shape, names, dtype, where="sbuf"):
@@ -26,7 +31,7 @@ SCRATCH.update(_s([128, 768], "OUTP TQ", "float32"))
 SCRATCH.update(_s([128, 4], "RT", "bfloat16"))
 SCRATCH.update(_s([128, 4], "RS", "float32"))
 SCRATCH.update(_s([128, 16], "BB PF", "float32"))
-SCRATCH.update(_s([128, 8], "ROW8 GS GB", "bfloat16"))
+SCRATCH.update(_s([128, 8], "GS GB", "bfloat16"))
 SCRATCH.update(_s([128, 16], "JM PI PQ", "int32"))
 SCRATCH.update(_s([128, 16], "J0 J1 VL OL", "uint16"))
 SCRATCH.update(_s([128, 1024], "PK Q M", "int32"))
@@ -36,15 +41,76 @@ SCRATCH.update(_s([128, 4096], "XG GD OV E", "bfloat16"))
 SCRATCH.update(_s([128, 4096], "GN", "float16"))
 SCRATCH.update(_s([128, 256], "A16 N16", "uint16"))
 SCRATCH.update(_s([128, 256], "AC NX CU CN UC NN NH MC G1 G2 G3 VR FE F3", "float16"))
-SCRATCH.update(_s([128, 256], "LJ WR HT H COND HH DL Y1 Y2 IXB B1 BIAS RST ROW16 MASK ONE NONE N1K", "bfloat16"))
+SCRATCH.update(_s([128, 256], "LJ WR HT H COND HH HS DL Y1 Y2 IXB B1 BIAS RST ROW16 MASK ONE NONE N1K", "bfloat16"))
 SCRATCH.update(_s([128, 256], "PM PX PV PO REC CM T1F T2F Q3F LAND3", "float32"))
 SCRATCH.update(_s([128, 256], "A32 EV IX ME T10 T20 T11 T21 LAND1 LAND2", "int32"))
-SCRATCH.update(_s([128, 144], "ROWC SH", "bfloat16"))
+SCRATCH.update(_s([128, 144], "SH", "bfloat16"))
 SCRATCH.update(_s([128, 128], "ID ZERO BLK NBLK BLKQ AVG " + " ".join(n for n, _ in SCALED), "bfloat16"))
 SCRATCH.update(_s([128, 512], "b0 b1 b2 b3 b4 b5 b6 b7", "float32", "psum"))
 DMAS = ["jt", "jm", "lm", "xw", "sd", "rt", "pk", "oq", "o3", "ox"]
 SEMAPHORES = ["sv", "sa", "st", "sg"] + ["d" + d for d in DMAS] + ["ar0", "ar1", "ar2", "lc0", "lc1", "lc2"]
-PSUM = ("b0", "b1", "b2", "b3", "b4", "b5", "b6", "b7")
+
+
+def bank(tag):
+    return tag[:2] if len(tag) == 3 and tag[0] == "b" and tag[2] in "lh" else None
+
+
+def order(calls):
+    n = len(calls)
+    after, before, wrote, read = [], [set() for _ in calls], {}, {}
+    for i, (q, _, _, R, W, _) in enumerate(calls):
+        W = W + [bank(x) + "#" for x in W if bank(x) and q == "t"]
+        after.append({wrote[x] for x in R + W if x in wrote} | {j for x in W for j in read.get(x, ())})
+        for j in after[i]:
+            before[j].add(i)
+        for x in R:
+            read.setdefault(x, []).append(i)
+        for x in W:
+            wrote[x], read[x] = i, []
+    banks = [{bank(x) for x in c[3] + c[4]} - {None} for c in calls]
+
+    def run(needs, users, urgency, back):
+        free, held, done, out = {}, {}, [0.0] * n, []
+        waiting, earliest = [len(a) for a in needs], [calls[i][5] if back else 0.0 for i in range(n)]
+        ready = {q: [i for i in range(n) if not needs[i] and calls[i][0] == q] for q in "vatgs"}
+        for _ in range(n):
+            best = None
+            for q in "vatgs":
+                can = sorted(((-i if q == "s" else urgency[i], i,
+                               max([free.get(q, 0.0), earliest[i]] + [held[b][1] + WAKE for b in banks[i] if b in held and held[b][0] != q]))
+                              for i in ready[q]), reverse=True)
+                if can:
+                    take = can[0]
+                    for c in can[1:]:
+                        if c[2] < take[2] and c[2] + calls[c[1]][2] <= take[2] + SLACK:
+                            take = c
+                    if best is None or take[2] < best[0]:
+                        best = (take[2], take[1], q)
+            s, i, q = best
+            done[i] = free[q] = s + calls[i][2]
+            for b in banks[i]:
+                held[b] = (q, free[q])
+            out.append(i)
+            ready[q].remove(i)
+            for j in users[i]:
+                earliest[j] = max(earliest[j], done[i] + calls[j if back else i][5] + (0 if q == "t" == calls[j][0] else WAKE))
+                waiting[j] -= 1
+                if waiting[j] == 0:
+                    ready[calls[j][0]].append(j)
+        return out, done
+    urgency = [0.0] * n
+    for i in reversed(range(n)):
+        urgency[i] += calls[i][2] + calls[i][5] + WAKE
+        for j in after[i]:
+            urgency[j] = max(urgency[j], urgency[i])
+    best = None
+    for _ in range(ROUNDS):
+        out, done = run(after, before, urgency, False)
+        end = max(done[i] + calls[i][5] for i in range(n))
+        if best is None or end < best[0]:
+            best = (end, out)
+        urgency = run(before, after, done, True)[1]
+    return best[1]
 
 
 def rank_program(g, core, T, topo):
@@ -54,82 +120,65 @@ def rank_program(g, core, T, topo):
     nxt = T.cores[(rank + 1) % len(T.cores)]
     prv = T.cores[(rank - 1) % len(T.cores)]
     queue = {"v": g.vector, "a": g.scalar, "t": g.tensor, "g": g, "s": g.sync}
-    count = {"sv": 0, "sa": 0, "st": 0, "sg": 0}
-    seen, wrote, readers = {}, {}, {}
+    calls, signals = [], {}
 
-    def emit(q, fn, R, W, sem=None, inc=1, total=None):
-        need = {}
+    def call(ways, R, W, delay=0.0, signal=None):
+        if signal:
+            signals[len(calls)] = signal
+        (q, (fn, ns)), = ways.items()
+        calls.append((q, fn, ns, R.split(), W.split(), delay))
 
-        def want(s, v):
-            if s == "st" and q == "t":
-                return
-            if need.get(s, 0) < v:
-                need[s] = v
-        own = "s" + q
-        for tag in R:
-            if tag in wrote:
-                want(*wrote[tag])
-            if tag in PSUM:
-                for s, v in readers.get(tag, {}).items():
-                    if s != own:
-                        want(s, v)
-        for tag in W:
-            if tag in wrote:
-                want(*wrote[tag])
-            for s, v in readers.get(tag, {}).items():
-                want(s, v)
-        for s in sorted(need):
-            if seen.get((q, s), 0) < need[s]:
-                queue[q].wait_ge(T.sem[s], need[s])
-                seen[(q, s)] = need[s]
-        ins = fn()
-        if sem is None:
-            sem = own
-            count[sem] += 1
-            total = count[sem]
-        if inc:
-            ins.then_inc(T.sem[sem], inc)
-        for tag in R:
-            readers.setdefault(tag, {})[sem] = total
-        for tag in W:
-            wrote[tag] = (sem, total)
-            readers[tag] = {}
+    def vector(n, per=1.0, way=None):
+        return CALL + (n * way if way else max(64, n * per) * CYCLE)
 
-    def V(R, W, fn):
-        emit("v", fn, R.split(), W.split())
+    def scalar(n, way=None):
+        return CALL + 20 + n * (way or CYCLE)
 
-    def D(q, name, R, W, out, in_):
-        emit(q, lambda: queue[q].dma_start(out=out, in_=in_), R.split(), W.split(), "d" + name, 16, 16)
+    def D(q, name, R, W, out, in_, delay):
+        call({q: (lambda: queue[q].dma_start(out=out, in_=in_), 50.0)}, R, W, delay, ("d" + name, 16, 16))
 
-    def act(R, W, out, in_, func=AF.Copy, bias=None, **kw):
-        if bias is not None:
-            i = [n for n, _ in BIASES].index(bias)
-            kw["bias"] = T.BB[:, i:i + 1]
-            R += " BB"
-            if func == AF.Copy:
-                func = AF.Identity
-        emit("a", lambda: g.scalar.activation(out=out, in_=in_, func=func, **kw), R.split(), W.split())
+    def activation(out, in_, func, bias, scale):
+        kw = {} if bias is None else {"bias": T.BB[:, BIASES.index(bias):BIASES.index(bias) + 1]}
+        if scale is not None:
+            kw["scale"] = scale
+        if func is None:
+            func = AF.Copy if bias is None else AF.Identity
+        return lambda: g.scalar.activation(out=out, in_=in_, func=func, **kw)
 
-    def mm(R, W, out, lhsT, rhs, start, stop):
-        emit("t", lambda: g.tensor.matmul(out=out, lhsT=lhsT, rhs=rhs, start=start, stop=stop), R.split(), W.split())
+    def biased(R, bias):
+        return R if bias is None else R + " BB%d" % BIASES.index(bias)
 
-    def cp(R, W, out, in_):
-        V(R, W, lambda: g.vector.tensor_copy(out=out, in_=in_))
+    def act(R, W, out, in_, func, bias=None, n=256):
+        call({"a": (activation(out, in_, func, bias, None), scalar(n))}, biased(R, bias), W)
 
-    def tt(R, W, out, in0, in1, op):
-        V(R, W, lambda: g.vector.tensor_tensor(out=out, in0=in0, in1=in1, op=op))
-
-    def ts(R, W, out, in0, s1, op0, s2=None, op1=None):
-        if op1 is None:
-            V(R, W, lambda: g.vector.tensor_scalar(out=out, in0=in0, scalar1=s1, scalar2=None, op0=op0))
+    def move(R, W, out, in_, scale=None, bias=None, n=256, per=1.0, way=None, on="a"):
+        if bias is None:
+            v = lambda: g.vector.tensor_copy(out=out, in_=in_)
+        elif scale is None:
+            v = lambda: g.vector.tensor_scalar(out=out, in0=in_, scalar1=bias, scalar2=None, op0=OP.add)
         else:
-            V(R, W, lambda: g.vector.tensor_scalar(out=out, in0=in0, scalar1=s1, scalar2=s2, op0=op0, op1=op1))
+            v = lambda: g.vector.tensor_scalar(out=out, in0=in_, scalar1=scale, scalar2=bias, op0=OP.mult, op1=OP.add)
+        ways = {"a": (activation(out, in_, None, bias, scale), scalar(n, way)), "v": (v, vector(n, per, way))}
+        call({on: ways[on]}, biased(R, bias) if on == "a" else R, W)
+
+    def mm(R, W, out, lhsT, rhs, start, stop, n):
+        call({"t": (lambda: g.tensor.matmul(out=out, lhsT=lhsT, rhs=rhs, start=start, stop=stop), max(64, n) * TENSOR)}, R, W)
+
+    def tt(R, W, out, in0, in1, op, n=256, per=1.0, way=None):
+        call({"v": (lambda: g.vector.tensor_tensor(out=out, in0=in0, in1=in1, op=op), vector(n, per, way))}, R, W)
+
+    def ts(R, W, out, in0, s1, op0, s2=None, op1=None, n=256, per=1.0, way=None):
+        kw = {} if op1 is None else {"op1": op1}
+        call({"v": (lambda: g.vector.tensor_scalar(out=out, in0=in0, scalar1=s1, scalar2=s2, op0=op0, **kw), vector(n, per, way))}, R, W)
 
     def scan(R, W, out, d0, d1, initial, op0, op1):
-        V(R, W, lambda: g.vector.tensor_tensor_scan(out=out, data0=d0, data1=d1, initial=initial, op0=op0, op1=op1))
+        call({"v": (lambda: g.vector.tensor_tensor_scan(out=out, data0=d0, data1=d1, initial=initial, op0=op0, op1=op1), vector(256))}, R, W)
 
-    def fill(W, ap, c):
-        V("", W, lambda: g.vector.memset(ap, c))
+    def scatter(R, W, out, in_):
+        call({"v": (lambda: g.vector.tensor_copy(out=out, in_=in_), vector(256, way=SCATTER))}, R, W)
+
+    def fill(W, ap, c, n=1):
+        call({"v": (lambda: g.vector.memset(ap, c), vector(n, 0.5))}, "", W)
 
     def part(name, i):
         return T[name][:, 256 * i:256 * i + 256]
@@ -144,355 +193,239 @@ def rank_program(g, core, T, topo):
             first, end = start and n == 0, stop and n == len(terms) - 1
             if w[0] == "~":
                 for h in range(2):
-                    mm(tag + " " + w[1:], place[:2], at(place, 128 * h, 128 * h + 128), T[tag][:, 128 * h:128 * h + 128], T[w[1:]][:], False, end and h == 1)
+                    mm(tag + " " + w[1:], place, at(place, 128 * h, 128 * h + 128), T[tag][:, 128 * h:128 * h + 128], T[w[1:]][:], False, end and h == 1, 128)
             else:
-                mm(tag + " " + w, place[:2], at(place), T[w][:], ap, first, end)
+                mm(tag + " " + w, place, at(place), T[w][:], ap, first, end, 256)
 
     def pick(place, what, h, tag, rhs, stop):
         tags = " ".join("%s%d" % (what, c) for c in range(4 * h, 4 * h + 4)) + " " + tag
         for k in range(16):
-            mm(tags, place[:2], at(place, 128 * h + k, 128 * h + 128, 16), T[what][:, 2048 * h + k:2048 * h + 2048:16], rhs(k), False, stop and k == 15)
+            mm(tags, place, at(place, 128 * h + k, 128 * h + 128, 16), T[what][:, 2048 * h + k:2048 * h + 2048:16], rhs(k), False, stop and k == 15, 8)
 
-    D("a", "jm", "", "JM", T.JM[:], T.jm[:])
-    D("s", "jt", "", "JT", T.JT[:], T.jt[:])
-    D("s", "xw", "", "X", T.X[:, 0:3072], T.xw[:])
-    D("s", "lm", "", "LM", T.LM[:], T.lm[:])
-    D("s", "sd", "", "SD", T.SD[:], T.sd[:])
-    D("s", "pk", "", "PK", T.PK[:], T.pk[:])
-    D("a", "rt", "", "RT", T.RT[:, 0:3], T.rt[:])
+    landed = 1600.0
+    for q, name, tag, out, in_, kib in (("a", "jm", "JM", T.JM[:], T.jm[:], 8), ("s", "jt", "JT", T.JT[:], T.jt[:], 384),
+                                        ("s", "xw", "X", T.X[:, 0:3072], T.xw[:], 768), ("s", "lm", "LM", T.LM[:], T.lm[:], 192),
+                                        ("s", "sd", "SD", T.SD[:], T.sd[:], 768), ("s", "pk", "PK", T.PK[:], T.pk[:], 512),
+                                        ("a", "rt", "RT", T.RT[:, 0:3], T.rt[:], 1)):
+        landed += 2.6 * kib
+        D(q, name, "", tag, out, in_, landed)
 
-    def iota(nm, pattern, base=0, cm=0, exact=True):
-        if exact:
-            emit("g", lambda: g.iota(T[nm][:], pattern, base, cm), [], [nm])
-        else:
-            emit("g", lambda: g.iota(T[nm][:], pattern, base, cm, allow_small_or_imprecise_dtypes=True), [], [nm])
+    def iota(nm, pattern, base=0, cm=0, n=256):
+        kw = {} if nm == "PI" else {"allow_small_or_imprecise_dtypes": True}
+        call({"g": (lambda: g.iota(T[nm][:], pattern, base, cm, **kw), 130 + 2 * n * CYCLE)}, "", nm)
 
-    def select(nm, src, pattern, op, x, base, cm):
-        emit("g", lambda: g.affine_select(T[nm][:], T[src][:], pattern, op, x, base, cm), [src], [nm])
-    iota("PI", [[0, 16]], 0, 1)
-    iota("ROWC", [[1, 144]], exact=False)
-    iota("ROW8", [[16, 8]], exact=False)
-    iota("ROW16", [[0, 16], [1, 16]], exact=False)
-    iota("CM", [[1, 256]], 9600, exact=False)
-    fill("ZERO", T.ZERO[:], 0.0)
-    for nm, x in SCALED:
+    def select(nm, src, pattern, op, x, base, cm, n=128):
+        call({"g": (lambda: g.affine_select(T[nm][:], T[src][:], pattern, op, x, base, cm), 170 + 2 * n * CYCLE)}, src, nm)
+
+    def own_group(nm, x, n, w):
+        iota(nm, [[0, n * w]], x, n=n * w)
+        select(nm, nm, [[-16, n], [0, w]], OP.is_ge, 0.0, 0, 1, n * w)
+        select(nm, nm, [[16, n], [0, w]], OP.is_ge, 0.0, 15, -1, n * w)
+    fill("ZERO", T.ZERO[:], 0.0, 128)
+    for i, x in enumerate(BIASES):
+        fill("BB%d" % i, T.BB[:, i:i + 1], x)
+    for nm, x in (("ONE", 1.0), ("AVG", 1.0 / 128), ("N1K", -1280.0), ("NONE", -1.0)):
+        fill(nm, T[nm][:], x, 256)
+    iota("PI", [[0, 16]], 0, 1, 16)
+    iota("ROW16", [[0, 16], [1, 16]])
+    iota("BIAS", [[0, 16], [-1, 16]], 15)
+    iota("CM", [[1, 256]], 5504)
+    select("RST", "ONE", [[0, 16], [1, 16]], OP.not_equal, 0.0, 0, 0, 256)
+    for nm, x in (("ID", 1.0),) + SCALED:
         select(nm, "ZERO", [[-1, 128]], OP.not_equal, x, 0, 1)
-    for i, (_, x) in enumerate(BIASES):
-        fill("BB", T.BB[:, i:i + 1], x)
-    for nm, x in (("ONE", 1.0), ("NONE", -1.0), ("N1K", -1280.0), ("AVG", 1.0 / 128)):
-        fill(nm, T[nm][:], x)
-    cp("PI", "PF", T.PF[:, 0:1], T.PI[:, 0:1])
-    ts("PI", "PQ", T.PQ[:, 0:1], T.PI[:, 0:1], 15, OP.bitwise_and)
-    ts("PI", "PQ", T.PQ[:, 1:2], T.PI[:, 0:1], 112, OP.bitwise_and)
-    cp("PQ", "PF", T.PF[:, 1:3], T.PQ[:, 0:2])
-    ts("ROWC PF", "ID", T.ID[:], T.ROWC[:, 0:128], T.PF[:, 0:1], OP.is_equal)
-    ts("ROW8 PF", "GB", T.GB[:], T.ROW8[:], T.PF[:, 2:3], OP.is_equal)
-    ts("GB", "GS", T.GS[:], T.GB[:], 16.0, OP.mult)
-    ts("ROW16", "BIAS", T.BIAS[:], T.ROW16[:], -1.0, OP.mult, 15.0, OP.add)
-    ts("ROW16", "RST", T.RST[:], T.ROW16[:], 0.0, OP.is_gt)
+    for nm, x, n, w in (("GB", 1, 8, 1), ("GS", 16, 8, 1), ("BLK", 1, 8, 16), ("NBLK", -1, 8, 16), ("BLKQ", 4096, 8, 16), ("SH", 1, 9, 16)):
+        own_group(nm, x, n, w)
+    select("SH", "SH", [[0, 9], [1, 16]], OP.is_equal, 0.0, -15, 0, 144)
+    ts("PI", "PQ", T.PQ[:, 0:1], T.PI[:, 0:1], 15, OP.bitwise_and, n=1)
+    move("PQ", "PF", T.PF[:, 0:1], T.PQ[:, 0:1], n=1, on="v")
+    ts("ROW16 PF", "MASK", T.MASK[:], T.ROW16[:], T.PF[:, 0:1], OP.not_equal, 8192.0, OP.mult, per=0.5)
+    tt("CM MASK", "CM", T.CM[:], T.CM[:], T.MASK[:], OP.subtract, per=2)
+    ts("RT", "RS", T.RS[:, 0:3], T.RT[:, 0:3], 8.0, OP.add, n=3)
 
-    def late_constants():
-        ts("ROWC PF", "SH", T.SH[:], T.ROWC[:], -15.0, OP.add, T.PF[:, 2:3], OP.is_equal)
-        ts("ROWC ROW16", "BLK", T.BLK[:], T.ROW16[:, 0:128], -1.0, OP.mult)
-        tt("ROWC BLK", "BLK", T.BLK[:], T.ROWC[:, 0:128], T.BLK[:], OP.add)
-        ts("BLK PF", "NBLK", T.NBLK[:], T.BLK[:], T.PF[:, 2:3], OP.is_equal, -1.0, OP.mult)
-        ts("BLK PF", "BLKQ", T.BLKQ[:], T.BLK[:], T.PF[:, 2:3], OP.is_equal, 4096.0, OP.mult)
-        ts("BLK PF", "BLK", T.BLK[:], T.BLK[:], T.PF[:, 2:3], OP.is_equal)
-        ts("ROW16 PF", "MASK", T.MASK[:], T.ROW16[:], T.PF[:, 1:2], OP.not_equal, 8192.0, OP.mult)
-        ts("ROW16 PF", "b7", at("b7l"), T.ROW16[:], T.PF[:, 1:2], OP.is_equal)
-        tt("CM b7", "b7", at("b7l"), T.CM[:], at("b7l"), OP.mult)
-        ts("b7", "CM", T.CM[:], at("b7l"), -4096.0, OP.add)
-        ts("RT", "RS", T.RS[:, 0:3], T.RT[:, 0:3], 8.0, OP.add)
-
-    def tools(t):
-        J = "J%d" % (t % 2)
-        ts("JT " + J, "A32", T.A32[:], T.JT[:].indirect(T[J][:]), 4095, OP.bitwise_and)
-        cp("A32", "A16", T.A16[:], T.A32[:])
-
-    def nexts(t):
-        J = "J%d" % (t % 2)
-        act("JT " + J, "NX", T.NX[:], T.JT[:].indirect(T[J][:]), bias="job", scale=1.0 / 4096)
-
-    def forms():
-        ts("NX", "N16", T.N16[:], T.NX[:], -1280.0, OP.add)
-        ts("A16", "AC", T.AC[:], T.A16[:], -1664.0, OP.add)
-
-    def limits(t):
-        J = "J%d" % (t % 2)
-        act("LM " + J, "LJ", T.LJ[:], T.LM[:].indirect(T[J][:]))
-
-    def gather(what, q, cs):
-        s, w = slice(32 * cs[0], 32 * cs[-1] + 32), slice(512 * cs[0], 512 * cs[-1] + 512)
-        W = " ".join("%s%d" % (what, c) for c in cs)
-        if what == "GN":
-            src = T.JT[:].indirect(T.N16[:, s])
-            if q == "a":
-                act("JT N16", W, T.GN[:, w], src, bias="job", scale=1.0 / 4096)
+    def gather(what, mine):
+        for c in range(0, 8, PIECE):
+            s, w = slice(32 * c, 32 * (c + PIECE)), slice(512 * c, 512 * (c + PIECE))
+            W, on = " ".join("%s%d" % (what, x) for x in range(c, c + PIECE)), "v" if c in mine else "a"
+            if what == "GN":
+                move("JT N16", W, T.GN[:, w], T.JT[:].indirect(T.N16[:, s]), 1.0 / 4096, JOB, 512 * PIECE, way=GATHER, on=on)
             else:
-                ts("JT N16", W, T.GN[:, w], src, 1.0 / 4096, OP.mult, 1279.625, OP.add)
-        else:
-            tab = "X" if what == "XG" else "SD"
-            (act if q == "a" else cp)(tab + " A16", W, T[what][:, w], T[tab][:, 0:3072].indirect(T.A16[:, s]))
-
-    def diagonal(place, what, h, first=None, stop=True):
-        if first:
-            mm(first[0] + " " + first[1], place[:2], at(place, 128 * h, 128 * h + 128), T[first[0]][:, 128 * h:128 * h + 128], T[first[1]][:], True, False)
-        pick(place, what, h, "ID", lambda k: T.ID[:, k::16], stop)
-
-    def sisters(h):
-        diagonal("b0l", "GD", h, ("AC", "ID"))
-
-    def wraps():
-        act("b0", "WR", T.WR[:], at("b0l"), AF.Sign, bias="wrap")
-        add("b0h", [("IW", "WR")], start=True)
-        for h in range(2):
-            diagonal("b0h", "GD", h, None, h == 1)
-
-    def seconds(h):
-        diagonal("b1l", "GN", h, ("NX", "NID"))
-
-    def sums(h):
-        if h == 0:
-            add("b3l", [("ID", "LJ")], True, True)
-            add("b3h", [("AVG", "BIAS")], True)
-        pick("b3h", "XG", h, "GS", lambda k: T.GS[:], h == 1)
-
-    def heavy():
-        scan("RST b3", "PM", T.PM[:], T.RST[:], at("b3h"), 0.0, OP.mult, OP.max)
-        scan("RST PM", "PX", T.PX[:, ::-1], T.RST[:], T.PM[:, ::-1], 0.0, OP.mult, OP.max)
-        tt("PX b3", "HT", T.HT[:], T.PX[:], at("b3h"), OP.is_equal)
-        for h in range(2):
-            mm("HT ID", "b4", T.b4[:, 128 * h:128 * h + 128], T.HT[:, 128 * h:128 * h + 128], T.ID[:], True, True)
-
-    def heavy_a():
-        act("b4", "H", T.H[:], at("b4l"))
-
-    def compare(ks):
-        for k in ks:
-            tt(" ".join("XG%d" % c for c in range(8)) + " b3", "OV%d" % k, part("OV", k), T.XG[:, k::16], at("b3l"), OP.is_gt)
-            for h in range(2):
-                mm("OV%d GB" % k, "b2", T.b2[:, 128 * h + k:128 * h + 128:16], T.OV[:, 256 * k + 128 * h:256 * k + 128 * h + 128], T.GB[:], True, True)
-
-    def pocket3(t):
-        return ("Q3", part("Q", 3)) if t == 0 else ("LAND%d" % t, T["LAND%d" % t][:])
-
-    def init_pockets_a():
-        act("PK", "FH", T.FH[:], T.PK[:], bias="job", scale=1.0 / 4096)
-        for i, (place, bits) in enumerate((("b6l", "IF"), ("b6h", "I8"), ("b7l", "I4"), ("b7h", None))):
-            add(place, [("IF", ("FH", part("FH", i))), ("IF", "N1K")] + ([(bits, "ONE")] if bits else []), True, True)
-
-    def init_pockets():
-        ts("PK", "M0 M1 M2 M3", T.M[:], T.PK[:], 4095, OP.bitwise_and)
-        for b, s in (("b6", slice(0, 512)), ("b7", slice(512, 1024))):
-            tt("PK " + b, "Q0 Q1" if b == "b6" else "Q2 Q3", T.Q[:, s], T.PK[:, s], T[b][:], OP.add)
-
-    def victims(t):
-        q3, l3 = pocket3(t)
-        tt("Q0 Q1", "b2", at("b2h"), part("Q", 0), part("Q", 1), OP.max)
-        tt("Q2 b2", "b2", at("b2h"), part("Q", 2), at("b2h"), OP.max)
-        tt(q3 + " b2", "EV", T.EV[:], l3, at("b2h"), OP.max)
-        if t:
-            ts(q3, "M3", part("M", 3), l3, 4095, OP.bitwise_and)
-        ts("EV", "ME", T.ME[:], T.EV[:], 4095, OP.bitwise_and)
-        ts("EV", "IX", T.IX[:], T.EV[:], 12, OP.logical_shift_right, 3, OP.bitwise_and)
-
-    def victims_a():
-        act("ME", "MC", T.MC[:], T.ME[:], bias="name")
-        act("IX", "IXB", T.IXB[:], T.IX[:])
-        act("IX", "B1", T.B1[:], T.IX[:], AF.Sign, bias="bit")
-
-    banks = ("b0", "b1", "b5")
+                tab = "X" if what == "XG" else "SD"
+                move(tab + " A16", W, T[what][:, w], T[tab][:, 0:3072].indirect(T.A16[:, s]), n=512 * PIECE, way=GATHER, on=on)
 
     def eq(i):
         return ("EQ%d" % i, part("EQ", i))
 
-    def chosen(i):
-        terms = [(("ID", "NID", "ID")[i], "IXB")] + ([(("IK", "IW")[i - 1], "B1")] if i else [])
-        terms += [("I4" if j == i else "NID", eq(j)) for j in range(i, 4)] + [("NB", eq(j)) for j in range(i)]
-        add(banks[i] + "l", terms, True, True)
-        act(banks[i], "SG%d" % i, part("SG", i), at(banks[i] + "l"), AF.Sign, bias="s%d" % i)
-
-    def masks(i, last):
-        sg = ("SG%d" % i, part("SG", i))
-        if last:
-            add(banks[i] + "l", [("NF", ("FH", part("FH", i))), ("NB", sg), ("IM", "NONE"), (("IF", "I8", "I4")[i], "NONE")], True, True)
-            add(banks[i] + "h", [("I4", "NN"), ("IL", sg), ("IC", sg), ("ID", "UC")], True, True)
-        else:
-            add(banks[i] + "l", [("NB", sg)], True, True)
-            add(banks[i] + "h", [("IQ", "NN"), ("IB", sg), ("IP%d" % i, sg), ("ID", "UC")], True, True)
-
-    def update(last):
-        new = "OUTP" if last else "Q"
-        for i, b in enumerate(banks):
-            tt("Q%d " % i + b, "TQ%d" % i, part("TQ", i), part("Q", i), at(b + "l"), OP.add if last else OP.min)
-        for i, b in enumerate(banks):
-            tt("TQ%d " % i + b, new + str(i), part(new, i), part("TQ", i), at(b + "h"), OP.max)
-        if not last:
-            ts("Q0 Q1 Q2", "M0 M1 M2", T.M[:, 0:768], T.Q[:, 0:768], 4095, OP.bitwise_and)
-
-    def give_mask(t):
-        add("b0h", ([("NF", "FE"), ("NF", "N1K")] if t == 2 else []) + [("N4", "IXB")] + [("NB", eq(j)) for j in range(4)], True, True)
-
-    def give_pocket(t):
-        q3, l3 = ("Q3F", T.Q3F[:]) if t == 2 else pocket3(t)
-        t2 = "T2F" if t == 2 else "T2%d" % t
-        tt(q3 + " b2", t2, T[t2][:], l3, at("b2h"), OP.min)
-
-    def give(t):
-        t1, t2 = ("T1F", "T2F") if t == 2 else ("T1%d" % t, "T2%d" % t)
-        tt("EV b0", t1, T[t1][:], T.EV[:], at("b0h"), OP.add)
-        rid, pid = topo.addr(nxt)[0:2]
-        send = RemoteDMATransfer(dst_ids=[DstId(rid=rid, pnc=pid)], dma_engine_mask=topo.mask(core, nxt), remote_sem=T.sem["ar%d" % t],
-                                 srcs=[T[t1][:], T[t2][:]], dsts=[T["LAND%d" % (t + 1)][:]], alu_op=2)
-        emit("g", lambda: g.remote_dma_fused([send], local_sem=T.sem["lc%d" % t]), [t1, t2], [], "lc%d" % t, 0, len(topo.engines(core, nxt)))
-        wrote["LAND%d" % (t + 1)] = ("ar%d" % t, len(topo.engines(prv, core)))
-
-    def plain_forms():
-        act("EV", "FE", T.FE[:], T.EV[:], bias="key", scale=1.0 / 16384)
-        act("LAND2", "F3", T.F3[:], T.LAND2[:], bias="key", scale=1.0 / 16384)
-        act("Q0 Q1 Q2", "FH", T.FH[:, 0:768], T.Q[:, 0:768], bias="key", scale=1.0 / 16384)
-        add("b6l", [("NF", "F3"), ("NF", "N1K")], True, True)
-        tt("LAND2 b6", "Q3F", T.Q3F[:], T.LAND2[:], at("b6l"), OP.add)
-
-    cp("JM", "J0", T.J0[:], T.JM[:])
-    nexts(0)
-    tools(0)
-    forms()
-    gather("GN", "a", (0, 1))
-    gather("GN", "v", (2, 3))
-    gather("GN", "a", (4, 5))
-    late_constants()
-    limits(0)
-    gather("XG", "v", (0, 1))
-    gather("XG", "a", (4, 5))
-    gather("XG", "v", (2, 3))
-    gather("XG", "a", (6, 7))
-    seconds(0)
-    sums(0)
-    sums(1)
-    for c in (0, 2, 4):
-        gather("GD", "a", (c, c + 1))
-    heavy()
-    compare(range(8))
-    init_pockets_a()
-    gather("GD", "a", (6, 7))
-    sisters(0)
-    compare(range(8, 16))
-    sisters(1)
-    heavy_a()
-    wraps()
-    init_pockets()
-    victims(0)
-    victims_a()
+    move("PK", "FH", T.FH[:], T.PK[:], 1.0 / 4096, JOB, 1024)
+    ts("PK", "M0 M1 M2 M3", T.M[:], T.PK[:], 4095, OP.bitwise_and, n=1024)
+    for i, (place, bits) in enumerate((("b5l", "IF"), ("b5h", "I8"), ("b7l", "I4"), ("b7h", None))):
+        add(place, [("IF", ("FH", part("FH", i))), ("IF", "N1K")] + ([(bits, "ONE")] if bits else []), True, True)
+    tt("PK b5l b5h", "Q0 Q1", T.Q[:, 0:512], T.PK[:, 0:512], T.b5[:], OP.add, 512)
+    tt("PK b7l b7h", "Q2 Q3", T.Q[:, 512:1024], T.PK[:, 512:1024], T.b7[:], OP.add, 512)
+    move("JM", "J0", T.J0[:], T.JM[:], n=16, on="v")
 
     for t in range(3):
         last = t == 2
         J, J2 = "J%d" % (t % 2), "J%d" % ((t + 1) % 2)
-        add("b0l", [("ID", "AC"), ("IC", "ONE")], start=True)
-        add("b5l", [("ID", "MC")], True, True)
-        add("b3l", [("ID", "AC")], start=True)
-        add("b7l", [("ID", "MASK")], start=True)
-        ts("b2", "COND", T.COND[:], at("b2l"), 8.5, OP.is_gt)
-        tt("COND b0", "CU", T.CU[:], T.COND[:], at("b0h"), OP.mult)
-        add("b3l", [("~IW", "COND")])
-        add("b0l", [("~IW", "COND"), ("~ID", "CU")], stop=True)
-        add("b3l", [("~ID", "CU")], stop=True)
-        tt("H b5", "G1", T.G1[:], T.H[:], at("b5l"), OP.mult)
-        add("b7l", [("BLK", "G1")])
-        add("b6l", [("BLK", "G1")], start=True)
-        for cs in B1[t]:
-            gather("GN", "a", cs)
+        q3, l3 = ("Q3", part("Q", 3)) if t == 0 else ("LAND%d" % t, T["LAND%d" % t][:])
+        ts("JT " + J, "A32", T.A32[:], T.JT[:].indirect(T[J][:]), 4095, OP.bitwise_and, way=GATHER)
+        move("A32", "A16", T.A16[:], T.A32[:])
+        move("JT " + J, "NX", T.NX[:], T.JT[:].indirect(T[J][:]), 1.0 / 4096, JOB, way=GATHER)
+        move("NX", "N16", T.N16[:], T.NX[:], None, -1280.0, per=0.5, on="v")
+        move("A16", "AC", T.AC[:], T.A16[:], None, -1664.0, per=0.5, on="v")
+        move("LM " + J, "LJ", T.LJ[:], T.LM[:].indirect(T[J][:]), way=GATHER)
+        for what, mine in (("XG", VX), ("GD", VD), ("GN", VN)):
+            gather(what, mine[t])
+        tt("Q0 Q1", "b2h", at("b2h"), part("Q", 0), part("Q", 1), OP.max, per=2)
+        tt("Q2 b2h", "b2h", at("b2h"), part("Q", 2), at("b2h"), OP.max)
+        tt(q3 + " b2h", "EV", T.EV[:], l3, at("b2h"), OP.max)
         if t:
-            seconds(0)
+            ts(q3, "M3", part("M", 3), l3, 4095, OP.bitwise_and)
+        ts("EV", "ME", T.ME[:], T.EV[:], 4095, OP.bitwise_and)
+        ts("EV", "IX", T.IX[:], T.EV[:], 12, OP.logical_shift_right, 3, OP.bitwise_and)
+        move("ME", "MC", T.MC[:], T.ME[:], None, -1664.0)
+        move("IX", "IXB", T.IXB[:], T.IX[:])
+        act("IX", "B1", T.B1[:], T.IX[:], AF.Sign, -1.5)
+        if last:
+            move("LAND2", "F3", T.F3[:], T.LAND2[:], 1.0 / 16384, KEY)
+            move("EV", "FE", T.FE[:], T.EV[:], 1.0 / 16384, KEY)
+            move("Q0 Q1 Q2", "FH", T.FH[:, 0:768], T.Q[:, 0:768], 1.0 / 16384, KEY, 768)
+            add("b7h", [("NF", "F3"), ("NF", "N1K")], True, True)
+            tt("LAND2 b7h", "Q3F", T.Q3F[:], T.LAND2[:], at("b7h"), OP.add)
+            q3, l3 = "Q3F", T.Q3F[:]
+        add("b6l", [("AVG", "BIAS")], True)
+        for h in range(2):
+            pick("b6l", "XG", h, "GS", lambda k: T.GS[:], h == 1)
+        scan("RST b6l", "PM", T.PM[:], T.RST[:], at("b6l"), 0.0, OP.mult, OP.max)
+        scan("RST PM", "PX", T.PX[:, ::-1], T.RST[:], T.PM[:, ::-1], 0.0, OP.mult, OP.max)
+        tt("PX b6l", "HT", T.HT[:], T.PX[:], at("b6l"), OP.is_equal)
+        for h in range(2):
+            mm("HT ID", "b4l", at("b4l", 128 * h, 128 * h + 128), T.HT[:, 128 * h:128 * h + 128], T.ID[:], True, True, 128)
+        move("b4l", "H", T.H[:], at("b4l"))
+        for s in range(2):
+            mm("ID LJ", "b3l b3h", T.b3[:, s::2], T.ID[:], T.LJ[:], True, True, 256)
+        for k in range(8):
+            tt(" ".join("XG%d" % c for c in range(8)) + " b3l b3h", "OV%d" % k, T.OV[:, 512 * k:512 * k + 512], T.XG[:, k::8], T.b3[:], OP.is_gt, 512)
+            for s in range(2):
+                for h in range(2):
+                    o = 512 * k + 256 * h
+                    mm("OV%d GB" % k, "b2l", at("b2l", 128 * h + k + 8 * s, 128 * h + 128, 16), T.OV[:, o + s:o + 256:2], T.GB[:], True, True, 8)
+        ts("b2l", "COND", T.COND[:], at("b2l"), 8.5, OP.is_gt)
+        for h in range(2):
+            mm("AC ID", "b1h", at("b1h", 128 * h, 128 * h + 128), T.AC[:, 128 * h:128 * h + 128], T.ID[:], True, False, 128)
+            pick("b1h", "GD", h, "ID", lambda k: T.ID[:, k::16], True)
+        act("b1h", "WR", T.WR[:], at("b1h"), AF.Sign, -1407.5)
+        add("b0h", [("ZERO", "ONE")], start=True)
+        for h in range(2):
+            pick("b0h", "GD", h, "ID", lambda k: T.ID[:, k::16], False)
+        add("b0h", [("IW", "WR")], stop=True)
+        tt("COND b0h", "CU", T.CU[:], T.COND[:], at("b0h"), OP.mult)
+        add("b0l", [("ID", "AC"), ("IC", "ONE"), ("~IW", "COND"), ("~ID", "CU")], True, True)
+        add("b3l", [("ID", "AC"), ("~IW", "COND"), ("~ID", "CU")], True, True)
+        move("b3l", "UC", T.UC[:], at("b3l"))
         for i in range(4):
-            tt("M%d b0" % i, "EQ%d" % i, part("EQ", i), part("M", i), at("b0l"), OP.is_equal)
-            add("b2h", [("IB", eq(i))], i == 0, i == 3)
-        give_mask(t)
-        tt("H b2", "HH", T.HH[:], T.H[:], at("b2h"), OP.min)
-        give_pocket(t)
-        tt("HH b3", "G2", T.G2[:], T.HH[:], at("b3l"), OP.mult)
-        tt("HH b5", "G3", T.G3[:], T.HH[:], at("b5l"), OP.mult)
-        add("b7l", [("BLK", "G2")])
-        add("b6l", [("BLK", "G2"), ("NBLK", "G3")], stop=True)
-        add("b7l", [("NBLK", "G3")], stop=True)
+            tt("M%d b0l" % i, "EQ%d" % i, part("EQ", i), part("M", i), at("b0l"), OP.is_equal)
+        add("b2h", [("IB", eq(i)) for i in range(4)], True, True)
+        add("b5l", [("ID", "MC")], True, True)
+        tt("H b5l", "G1", T.G1[:], T.H[:], at("b5l"), OP.mult)
+        tt("H b2h", "HH", T.HH[:], T.H[:], at("b2h"), OP.min)
+        tt("HH b3l", "G2", T.G2[:], T.HH[:], at("b3l"), OP.mult)
+        tt("HH b5l", "G3", T.G3[:], T.HH[:], at("b5l"), OP.mult)
+        add("b6l", [("BLK", "G1"), ("BLK", "G2"), ("NBLK", "G3")], True, True)
+        add("b7l", [("ID", "MASK"), ("BLK", "G1"), ("BLK", "G2"), ("NBLK", "G3")], True, True)
         add("b4l", [("BLK", "HH")], True, True)
-        seconds(1)
-        add("b1h", [("ID", "NX")], start=True)
-        give(t)
-        act("b6", "VR", T.VR[:], at("b6l"))
-        scan("CM b7", "PV", T.PV[:], T.CM[:], at("b7l"), -4096.0, OP.max, OP.min)
-        act("b4 RS", "DL", T.DL[:], at("b4l"), bias="rest", scale=T.RS[:, t:t + 1])
-        act("b3", "UC", T.UC[:], at("b3l"))
-        if not last:
-            add("b4h", [("ID", "NX"), ("~IK", "HT")], start=True)
-        tt("COND b1", "CN", T.CN[:], T.COND[:], at("b1l"), OP.mult)
-        tt("PV b6", "E15", part("E", 15), T.PV[:], at("b6l"), OP.is_equal)
-        add("b1h", [("~ID", "CN")], stop=True)
-        act("b1", "NN", T.NN[:], at("b1h"), bias="next")
-        if not last:
-            add("b4h", [("~ID", "CN")], stop=True)
-            act("b4", "NH", T.NH[:], at("b4h"), AF.Relu, bias="next")
+        move("b6l", "VR", T.VR[:], at("b6l"))
+        move("b4l RS", "DL", T.DL[:], at("b4l"), T.RS[:, t:t + 1], -8.0)
+        scan("CM b7l", "PV", T.PV[:], T.CM[:], at("b7l"), -4096.0, OP.max, OP.min)
+        move("PV", "VL", T.VL[:], T.PV[:, 15::16], None, 1664.0, 16)
+        tt("PV b6l", "E15", part("E", 15), T.PV[:], at("b6l"), OP.is_equal)
         add("b7h", [("ID", "MASK"), ("ID", "VR"), ("BLKQ", ("E15", part("E", 15)))], start=True)
-        if not last:
-            add("b6h", [("I4", "NN"), ("ID", "UC")], True, True)
-            act("b6", "REC", T.REC[:], at("b6h"), bias="rec")
-            for r in range(16):
-                mm("NH SH", "b4", T.b4[:, 0:16], T.SH[:, 15 - r:143 - r], T.NH[:, r::16], r == 0, r == 15)
-            act("b4", J2, T[J2][:], T.b4[:, 0:16])
-        act("PV", "VL", T.VL[:], T.PV[:, 15::16], bias="list")
         for q in range(15):
-            ts("VR PV", "E%d" % q, T.E[:, 256 * q + 16 * q + 16:256 * q + 256], T.VR[:, 16 * q + 16:256], T.PV[:, 16 * q + 15:16 * q + 16], OP.is_equal)
-            mm("BLKQ E%d" % q, "b7", T.b7[:, 256 + 16 * q + 16:512], T.BLKQ[:], T.E[:, 256 * q + 16 * q + 16:256 * q + 256], False, q == 14)
-        if not last:
-            limits(t + 1)
-            cp("REC " + J, "JT", T.JT[:].indirect(T[J][:]), T.REC[:])
-        chosen(0)
-        chosen(1)
-        scan("CM b7", "PO", T.PO[:], T.CM[:], at("b7h"), -4096.0, OP.max, OP.min)
-        if not last:
-            tools(t + 1)
-            nexts(t + 1)
-        chosen(2)
-        tt("X VL DL", "Y1", T.Y1[:], T.X[:, 0:3072].indirect(T.VL[:]), T.DL[:], OP.add)
-        ts("PO", "OL", T.OL[:], T.PO[:, 15::16], -2432.0, OP.add)
-        ts("Y1", "Y2", T.Y2[:], T.Y1[:], 0.0, OP.max, 255.0, OP.min)
-        if not last:
-            for cs in B2:
-                gather("GD", "a", cs)
-            forms()
-        cp("Y2 OL", "X", T.X[:].indirect(T.OL[:]), T.Y2[:])
+            w = slice(256 * q + 16 * q + 16, 256 * q + 256)
+            ts("VR PV", "E%d" % q, T.E[:, w], T.VR[:, 16 * q + 16:256], T.PV[:, 16 * q + 15:16 * q + 16], OP.is_equal, n=240 - 16 * q, per=0.5)
+            mm("BLKQ E%d" % q, "b7h", at("b7h", 16 * q + 16), T.BLKQ[:], T.E[:, w], False, q == 14, 240 - 16 * q)
+        scan("CM b7h", "PO", T.PO[:], T.CM[:], at("b7h"), -4096.0, OP.max, OP.min)
+        move("PO", "OL", T.OL[:], T.PO[:, 15::16], None, -2432.0, 16, on="v")
+        tt("X VL DL", "Y1", T.Y1[:], T.X[:, 0:3072].indirect(T.VL[:]), T.DL[:], OP.add, way=GATHER)
+        ts("Y1", "Y2", T.Y2[:], T.Y1[:], 0.0, OP.max, 255.0, OP.min, per=0.5)
+        scatter("Y2 OL", "X", T.X[:].indirect(T.OL[:]), T.Y2[:])
         if last:
-            D("s", "ox", "X", "YX", T.yx[:, 0:3072], T.X[:, 0:3072])
+            D("s", "ox", "X", "YX", T.yx[:, 0:3072], T.X[:, 0:3072], 3600.0)
+        for h in range(2):
+            mm("NX NID", "b1l", at("b1l", 128 * h, 128 * h + 128), T.NX[:, 128 * h:128 * h + 128], T.NID[:], True, False, 128)
+            pick("b1l", "GN", h, "ID", lambda k: T.ID[:, k::16], True)
+        tt("COND b1l", "CN", T.CN[:], T.COND[:], at("b1l"), OP.mult)
+        add("b1h", [("ID", "NX"), ("~ID", "CN")], True, True)
+        move("b1h", "NN", T.NN[:], at("b1h"), None, -2304.0)
+        if not last:
+            add("b4h", [("ID", "NX"), ("~IK", "HT"), ("~ID", "CN")], True, True)
+            act("b4h", "NH", T.NH[:], at("b4h"), AF.Relu, -2304.0)
+            for r in range(16):
+                mm("NH SH", "b4h", at("b4h", 0, 16), T.SH[:, 15 - r:143 - r], T.NH[:, r::16], r == 0, r == 15, 16)
+            move("b4h", J2, T[J2][:], at("b4h", 0, 16), n=16)
+            add("b6h", [("I4", "NN"), ("ID", "UC")], True, True)
+            move("b6h", "REC", T.REC[:], at("b6h"), None, 4195968.0)
+            scatter("REC " + J, "JT", T.JT[:].indirect(T[J][:]), T.REC[:])
+        act("b2h", "HS", T.HS[:], at("b2h"), AF.Sign)
+        t1, t2 = ("T1F", "T2F") if last else ("T1%d" % t, "T2%d" % t)
+        tt(q3 + " b2h", t2, T[t2][:], l3, at("b2h"), OP.min)
+        add("b0h", ([("NF", "FE"), ("NF", "N1K")] if last else []) + [("N4", "IXB"), ("NB", "HS")], True, True)
+        tt("EV b0h", t1, T[t1][:], T.EV[:], at("b0h"), OP.add)
+        rid, pid = topo.addr(nxt)[0:2]
+        send = RemoteDMATransfer(dst_ids=[DstId(rid=rid, pnc=pid)], dma_engine_mask=topo.mask(core, nxt), remote_sem=T.sem["ar%d" % t],
+                                 srcs=[T[t1][:], T[t2][:]], dsts=[T["LAND%d" % (t + 1)][:]], alu_op=2)
+        call({"g": (lambda send=send, t=t: g.remote_dma_fused([send], local_sem=T.sem["lc%d" % t]), 300.0)}, t1 + " " + t2, "LAND%d" % (t + 1), 5000.0 if t else 7000.0,
+             ("lc%d" % t, 0, len(topo.engines(core, nxt)), "ar%d" % t, len(topo.engines(prv, core))))
+        old, new = ("b5l", "b5h", "b3l"), ("b0l", "b0h", "b3h")
         for i in range(3):
-            masks(i, last)
-        if last:
-            update(last)
-            D("s", "oq", "OUTP0 OUTP1 OUTP2", "YP", T.yp[:, 0:768], T.OUTP[:])
-            D("a", "o3", "LAND3", "YP3", T.yp[:, 768:1024], T.LAND3[:])
-            break
-        for c in (0, 2, 4, 6):
-            gather("XG", "a", (c, c + 1))
-        for what, cs in AV:
-            gather(what, "v", cs)
-        update(last)
-        sums(0)
-        victims(t + 1)
-        sums(1)
-        for cs in A1:
-            gather("GD", "a", cs)
-        heavy()
-        compare(range(6))
-        sisters(0)
-        victims_a()
-        heavy_a()
-        compare(range(6, 11))
-        sisters(1)
-        wraps()
-        for cs in A2:
-            gather("GN", "a", cs)
-        compare(range(11, 16))
-        if t == 1:
-            plain_forms()
+            terms = [(("ID", "NID", "ID")[i], "IXB")] + ([(("I5", "N2")[i - 1], "B1")] if i else [])
+            add(old[i], terms + [("I4", eq(i)), ("NID", "HS")] + [("NB", eq(j)) for j in range(i)], True, True)
+        act("b5l b5h", "SG0 SG1", T.SG[:, 0:512], T.b5[:], AF.Sign, -2.5, 512)
+        act("b3l", "SG2", part("SG", 2), at("b3l"), AF.Sign, -2.5)
+        for i in range(3):
+            sg = ("SG%d" % i, part("SG", i))
+            if last:
+                add(old[i], [("NF", ("FH", part("FH", i))), ("NB", sg), ("IM", "NONE"), (("IF", "I8", "I4")[i], "NONE")], True, True)
+                add(new[i], [("I4", "NN"), ("IL", sg), ("IC", sg), ("ID", "UC")], True, True)
+            else:
+                add(old[i], [("NB", sg)], True, True)
+                add(new[i], [("IQ", "NN"), ("IB", sg), ("IP%d" % i, sg), ("ID", "UC")], True, True)
+        to, op = ("OUTP", OP.add) if last else ("Q", OP.min)
+        tt("Q0 Q1 b5l b5h", "TQ0", T.TQ[:, 0:512], T.Q[:, 0:512], T.b5[:], op, 512)
+        tt("Q2 b3l", "TQ2", part("TQ", 2), part("Q", 2), at("b3l"), op)
+        tt("TQ0 b0l b0h", to + "0 " + to + "1", T[to][:, 0:512], T.TQ[:, 0:512], T.b0[:], OP.max, 512)
+        tt("TQ2 b3h", to + "2", part(to, 2), part("TQ", 2), at("b3h"), OP.max)
+        if not last:
+            ts("Q0 Q1 Q2", "M0 M1 M2", T.M[:, 0:768], T.Q[:, 0:768], 4095, OP.bitwise_and, n=768)
+    D("s", "oq", "OUTP0 OUTP1 OUTP2", "YP", T.yp[:, 0:768], T.OUTP[:], 2600.0)
+    D("a", "o3", "LAND3", "YP3", T.yp[:, 768:1024], T.LAND3[:], 2000.0)
+
+    count = {"sv": 0, "sa": 0, "st": 0, "sg": 0}
+    seen, wrote, readers = {}, {}, {}
+    for i in order(calls):
+        q = calls[i][0]
+        R, W = ({bank(x) or x for x in tags} for tags in calls[i][3:5])
+        own, need = "s" + q, {}
+        for tag in R | W:
+            before = [wrote[tag]] if tag in wrote else []
+            before += [(s, v) for s, v in readers.get(tag, {}).items() if tag in W or bank(tag + "l") and s != own]
+            for s, v in before:
+                if not s == "st" == own:
+                    need[s] = max(need.get(s, 0), v)
+        for s in sorted(need):
+            if seen.get((q, s), 0) < need[s]:
+                queue[q].wait_ge(T.sem[s], need[s])
+                seen[(q, s)] = need[s]
+        ins = calls[i][1]()
+        if i not in signals:
+            count[own] += 1
+        sem, inc, total = signals[i][:3] if i in signals else (own, 1, count[own])
+        if inc:
+            ins.then_inc(T.sem[sem], inc)
+        for tag in R:
+            readers.setdefault(tag, {})[sem] = total
+        for tag in W:
+            wrote[tag] = tuple(signals[i][3:]) if i in signals and not inc else (sem, total)
+            readers[tag] = {}
     for s in ("sv", "sa", "st", "sg"):
         g.wait_ge(T.sem[s], count[s])
     for d in DMAS:

from concourse.bass import DstId, RemoteDMATransfer
from concourse.mybir import AluOpType, ActivationFunctionType

OP = AluOpType
AF = ActivationFunctionType
BIG = 16777216.0
CYCLE, TENSOR, GATHER, SCATTER, CALL, WAKE = 0.83, 0.42, 1.2, 3.2, 45.0, 60.0
SLACK = 300.0
ROUNDS = 4
PIECE = 2
VX = ((0, 1, 2, 3), (6, 7), (6, 7))
VN = ((0, 1), (), ())
VD = ((), (), ())
SCALED = (("NID", -1.0), ("IF", 12288.0), ("I8", 8192.0), ("I4", 4096.0), ("IW", -1536.0), ("IC", 1664.0), ("IB", BIG), ("IK", 1024.0),
          ("N4", -4096.0), ("NB", -BIG), ("I5", 5.0), ("N2", -2.0), ("IQ", 16384.0), ("IP0", 13952.0), ("IP1", 9856.0), ("IP2", 5760.0),
          ("NF", -12288.0), ("IL", 4194304.0), ("IM", 1048576.0))
JOB, KEY = 1279.625, 1279.53125
BIASES = (JOB, KEY, -1280.0, -1407.5, -1664.0, -2304.0, 4195968.0, 1664.0, -8.0, -1.5, -2.5, -2432.0)


def _s(shape, names, dtype, where="sbuf"):
    return {n: (where, shape, dtype) for n in names.split()}


SCRATCH = {}
SCRATCH.update(_s([128, 3328], "X", "bfloat16"))
SCRATCH.update(_s([128, 3072], "SD", "bfloat16"))
SCRATCH.update(_s([128, 768], "JT", "int32"))
SCRATCH.update(_s([128, 768], "LM SG", "bfloat16"))
SCRATCH.update(_s([128, 768], "OUTP TQ", "float32"))
SCRATCH.update(_s([128, 4], "RT", "bfloat16"))
SCRATCH.update(_s([128, 4], "RS", "float32"))
SCRATCH.update(_s([128, 16], "BB PF", "float32"))
SCRATCH.update(_s([128, 8], "GS GB", "bfloat16"))
SCRATCH.update(_s([128, 16], "JM PI PQ", "int32"))
SCRATCH.update(_s([128, 16], "J0 J1 VL OL", "uint16"))
SCRATCH.update(_s([128, 1024], "PK Q M", "int32"))
SCRATCH.update(_s([128, 1024], "EQ", "bfloat16"))
SCRATCH.update(_s([128, 1024], "FH", "float16"))
SCRATCH.update(_s([128, 4096], "XG GD OV E", "bfloat16"))
SCRATCH.update(_s([128, 4096], "GN", "float16"))
SCRATCH.update(_s([128, 256], "A16 N16", "uint16"))
SCRATCH.update(_s([128, 256], "AC NX CU CN UC NN NH MC G1 G2 G3 VR FE F3", "float16"))
SCRATCH.update(_s([128, 256], "LJ WR HT H COND HH HS DL Y1 Y2 IXB B1 BIAS RST ROW16 MASK ONE NONE N1K", "bfloat16"))
SCRATCH.update(_s([128, 256], "PM PX PV PO REC CM T1F T2F Q3F LAND3", "float32"))
SCRATCH.update(_s([128, 256], "A32 EV IX ME T10 T20 T11 T21 LAND1 LAND2", "int32"))
SCRATCH.update(_s([128, 144], "SH", "bfloat16"))
SCRATCH.update(_s([128, 128], "ID ZERO BLK NBLK BLKQ AVG " + " ".join(n for n, _ in SCALED), "bfloat16"))
SCRATCH.update(_s([128, 512], "b0 b1 b2 b3 b4 b5 b6 b7", "float32", "psum"))
DMAS = ["jt", "jm", "lm", "xw", "sd", "rt", "pk", "oq", "o3", "ox"]
SEMAPHORES = ["sv", "sa", "st", "sg"] + ["d" + d for d in DMAS] + ["ar0", "ar1", "ar2", "lc0", "lc1", "lc2"]


def bank(tag):
    return tag[:2] if len(tag) == 3 and tag[0] == "b" and tag[2] in "lh" else None


def order(calls):
    n = len(calls)
    after, before, wrote, read = [], [set() for _ in calls], {}, {}
    for i, (q, _, _, R, W, _) in enumerate(calls):
        W = W + [bank(x) + "#" for x in W if bank(x) and q == "t"]
        after.append({wrote[x] for x in R + W if x in wrote} | {j for x in W for j in read.get(x, ())})
        for j in after[i]:
            before[j].add(i)
        for x in R:
            read.setdefault(x, []).append(i)
        for x in W:
            wrote[x], read[x] = i, []
    banks = [{bank(x) for x in c[3] + c[4]} - {None} for c in calls]

    def run(needs, users, urgency, back):
        free, held, done, out = {}, {}, [0.0] * n, []
        waiting, earliest = [len(a) for a in needs], [calls[i][5] if back else 0.0 for i in range(n)]
        ready = {q: [i for i in range(n) if not needs[i] and calls[i][0] == q] for q in "vatgs"}
        for _ in range(n):
            best = None
            for q in "vatgs":
                can = sorted(((-i if q == "s" else urgency[i], i,
                               max([free.get(q, 0.0), earliest[i]] + [held[b][1] + WAKE for b in banks[i] if b in held and held[b][0] != q]))
                              for i in ready[q]), reverse=True)
                if can:
                    take = can[0]
                    for c in can[1:]:
                        if c[2] < take[2] and c[2] + calls[c[1]][2] <= take[2] + SLACK:
                            take = c
                    if best is None or take[2] < best[0]:
                        best = (take[2], take[1], q)
            s, i, q = best
            done[i] = free[q] = s + calls[i][2]
            for b in banks[i]:
                held[b] = (q, free[q])
            out.append(i)
            ready[q].remove(i)
            for j in users[i]:
                earliest[j] = max(earliest[j], done[i] + calls[j if back else i][5] + (0 if q == "t" == calls[j][0] else WAKE))
                waiting[j] -= 1
                if waiting[j] == 0:
                    ready[calls[j][0]].append(j)
        return out, done
    urgency = [0.0] * n
    for i in reversed(range(n)):
        urgency[i] += calls[i][2] + calls[i][5] + WAKE
        for j in after[i]:
            urgency[j] = max(urgency[j], urgency[i])
    best = None
    for _ in range(ROUNDS):
        out, done = run(after, before, urgency, False)
        end = max(done[i] + calls[i][5] for i in range(n))
        if best is None or end < best[0]:
            best = (end, out)
        urgency = run(before, after, done, True)[1]
    return best[1]


def rank_program(g, core, T, topo):
    rank = T.rank_of(core)
    if rank is None:
        return
    nxt = T.cores[(rank + 1) % len(T.cores)]
    prv = T.cores[(rank - 1) % len(T.cores)]
    queue = {"v": g.vector, "a": g.scalar, "t": g.tensor, "g": g, "s": g.sync}
    calls, signals = [], {}

    def call(ways, R, W, delay=0.0, signal=None):
        if signal:
            signals[len(calls)] = signal
        (q, (fn, ns)), = ways.items()
        calls.append((q, fn, ns, R.split(), W.split(), delay))

    def vector(n, per=1.0, way=None):
        return CALL + (n * way if way else max(64, n * per) * CYCLE)

    def scalar(n, way=None):
        return CALL + 20 + n * (way or CYCLE)

    def D(q, name, R, W, out, in_, delay):
        call({q: (lambda: queue[q].dma_start(out=out, in_=in_), 50.0)}, R, W, delay, ("d" + name, 16, 16))

    def activation(out, in_, func, bias, scale):
        kw = {} if bias is None else {"bias": T.BB[:, BIASES.index(bias):BIASES.index(bias) + 1]}
        if scale is not None:
            kw["scale"] = scale
        if func is None:
            func = AF.Copy if bias is None else AF.Identity
        return lambda: g.scalar.activation(out=out, in_=in_, func=func, **kw)

    def biased(R, bias):
        return R if bias is None else R + " BB%d" % BIASES.index(bias)

    def act(R, W, out, in_, func, bias=None, n=256):
        call({"a": (activation(out, in_, func, bias, None), scalar(n))}, biased(R, bias), W)

    def move(R, W, out, in_, scale=None, bias=None, n=256, per=1.0, way=None, on="a"):
        if bias is None:
            v = lambda: g.vector.tensor_copy(out=out, in_=in_)
        elif scale is None:
            v = lambda: g.vector.tensor_scalar(out=out, in0=in_, scalar1=bias, scalar2=None, op0=OP.add)
        else:
            v = lambda: g.vector.tensor_scalar(out=out, in0=in_, scalar1=scale, scalar2=bias, op0=OP.mult, op1=OP.add)
        ways = {"a": (activation(out, in_, None, bias, scale), scalar(n, way)), "v": (v, vector(n, per, way))}
        call({on: ways[on]}, biased(R, bias) if on == "a" else R, W)

    def mm(R, W, out, lhsT, rhs, start, stop, n):
        call({"t": (lambda: g.tensor.matmul(out=out, lhsT=lhsT, rhs=rhs, start=start, stop=stop), max(64, n) * TENSOR)}, R, W)

    def tt(R, W, out, in0, in1, op, n=256, per=1.0, way=None):
        call({"v": (lambda: g.vector.tensor_tensor(out=out, in0=in0, in1=in1, op=op), vector(n, per, way))}, R, W)

    def ts(R, W, out, in0, s1, op0, s2=None, op1=None, n=256, per=1.0, way=None):
        kw = {} if op1 is None else {"op1": op1}
        call({"v": (lambda: g.vector.tensor_scalar(out=out, in0=in0, scalar1=s1, scalar2=s2, op0=op0, **kw), vector(n, per, way))}, R, W)

    def scan(R, W, out, d0, d1, initial, op0, op1):
        call({"v": (lambda: g.vector.tensor_tensor_scan(out=out, data0=d0, data1=d1, initial=initial, op0=op0, op1=op1), vector(256))}, R, W)

    def scatter(R, W, out, in_):
        call({"v": (lambda: g.vector.tensor_copy(out=out, in_=in_), vector(256, way=SCATTER))}, R, W)

    def fill(W, ap, c, n=1):
        call({"v": (lambda: g.vector.memset(ap, c), vector(n, 0.5))}, "", W)

    def part(name, i):
        return T[name][:, 256 * i:256 * i + 256]

    def at(place, a=0, b=256, step=1):
        o = 256 * "lh".index(place[2])
        return T[place[:2]][:, o + a:o + b:step]

    def add(place, terms, start=False, stop=False):
        for n, (w, x) in enumerate(terms):
            tag, ap = (x, T[x][:]) if isinstance(x, str) else x
            first, end = start and n == 0, stop and n == len(terms) - 1
            if w[0] == "~":
                for h in range(2):
                    mm(tag + " " + w[1:], place, at(place, 128 * h, 128 * h + 128), T[tag][:, 128 * h:128 * h + 128], T[w[1:]][:], False, end and h == 1, 128)
            else:
                mm(tag + " " + w, place, at(place), T[w][:], ap, first, end, 256)

    def pick(place, what, h, tag, rhs, stop):
        tags = " ".join("%s%d" % (what, c) for c in range(4 * h, 4 * h + 4)) + " " + tag
        for k in range(16):
            mm(tags, place, at(place, 128 * h + k, 128 * h + 128, 16), T[what][:, 2048 * h + k:2048 * h + 2048:16], rhs(k), False, stop and k == 15, 8)

    landed = 1600.0
    for q, name, tag, out, in_, kib in (("a", "jm", "JM", T.JM[:], T.jm[:], 8), ("s", "jt", "JT", T.JT[:], T.jt[:], 384),
                                        ("s", "xw", "X", T.X[:, 0:3072], T.xw[:], 768), ("s", "lm", "LM", T.LM[:], T.lm[:], 192),
                                        ("s", "sd", "SD", T.SD[:], T.sd[:], 768), ("s", "pk", "PK", T.PK[:], T.pk[:], 512),
                                        ("a", "rt", "RT", T.RT[:, 0:3], T.rt[:], 1)):
        landed += 2.6 * kib
        D(q, name, "", tag, out, in_, landed)

    def iota(nm, pattern, base=0, cm=0, n=256):
        kw = {} if nm == "PI" else {"allow_small_or_imprecise_dtypes": True}
        call({"g": (lambda: g.iota(T[nm][:], pattern, base, cm, **kw), 130 + 2 * n * CYCLE)}, "", nm)

    def select(nm, src, pattern, op, x, base, cm, n=128):
        call({"g": (lambda: g.affine_select(T[nm][:], T[src][:], pattern, op, x, base, cm), 170 + 2 * n * CYCLE)}, src, nm)

    def own_group(nm, x, n, w):
        iota(nm, [[0, n * w]], x, n=n * w)
        select(nm, nm, [[-16, n], [0, w]], OP.is_ge, 0.0, 0, 1, n * w)
        select(nm, nm, [[16, n], [0, w]], OP.is_ge, 0.0, 15, -1, n * w)
    fill("ZERO", T.ZERO[:], 0.0, 128)
    for i, x in enumerate(BIASES):
        fill("BB%d" % i, T.BB[:, i:i + 1], x)
    for nm, x in (("ONE", 1.0), ("AVG", 1.0 / 128), ("N1K", -1280.0), ("NONE", -1.0)):
        fill(nm, T[nm][:], x, 256)
    iota("PI", [[0, 16]], 0, 1, 16)
    iota("ROW16", [[0, 16], [1, 16]])
    iota("BIAS", [[0, 16], [-1, 16]], 15)
    iota("CM", [[1, 256]], 5504)
    select("RST", "ONE", [[0, 16], [1, 16]], OP.not_equal, 0.0, 0, 0, 256)
    for nm, x in (("ID", 1.0),) + SCALED:
        select(nm, "ZERO", [[-1, 128]], OP.not_equal, x, 0, 1)
    for nm, x, n, w in (("GB", 1, 8, 1), ("GS", 16, 8, 1), ("BLK", 1, 8, 16), ("NBLK", -1, 8, 16), ("BLKQ", 4096, 8, 16), ("SH", 1, 9, 16)):
        own_group(nm, x, n, w)
    select("SH", "SH", [[0, 9], [1, 16]], OP.is_equal, 0.0, -15, 0, 144)
    ts("PI", "PQ", T.PQ[:, 0:1], T.PI[:, 0:1], 15, OP.bitwise_and, n=1)
    move("PQ", "PF", T.PF[:, 0:1], T.PQ[:, 0:1], n=1, on="v")
    ts("ROW16 PF", "MASK", T.MASK[:], T.ROW16[:], T.PF[:, 0:1], OP.not_equal, 8192.0, OP.mult, per=0.5)
    tt("CM MASK", "CM", T.CM[:], T.CM[:], T.MASK[:], OP.subtract, per=2)
    ts("RT", "RS", T.RS[:, 0:3], T.RT[:, 0:3], 8.0, OP.add, n=3)

    def gather(what, mine):
        for c in range(0, 8, PIECE):
            s, w = slice(32 * c, 32 * (c + PIECE)), slice(512 * c, 512 * (c + PIECE))
            W, on = " ".join("%s%d" % (what, x) for x in range(c, c + PIECE)), "v" if c in mine else "a"
            if what == "GN":
                move("JT N16", W, T.GN[:, w], T.JT[:].indirect(T.N16[:, s]), 1.0 / 4096, JOB, 512 * PIECE, way=GATHER, on=on)
            else:
                tab = "X" if what == "XG" else "SD"
                move(tab + " A16", W, T[what][:, w], T[tab][:, 0:3072].indirect(T.A16[:, s]), n=512 * PIECE, way=GATHER, on=on)

    def eq(i):
        return ("EQ%d" % i, part("EQ", i))

    move("PK", "FH", T.FH[:], T.PK[:], 1.0 / 4096, JOB, 1024)
    ts("PK", "M0 M1 M2 M3", T.M[:], T.PK[:], 4095, OP.bitwise_and, n=1024)
    for i, (place, bits) in enumerate((("b5l", "IF"), ("b5h", "I8"), ("b7l", "I4"), ("b7h", None))):
        add(place, [("IF", ("FH", part("FH", i))), ("IF", "N1K")] + ([(bits, "ONE")] if bits else []), True, True)
    tt("PK b5l b5h", "Q0 Q1", T.Q[:, 0:512], T.PK[:, 0:512], T.b5[:], OP.add, 512)
    tt("PK b7l b7h", "Q2 Q3", T.Q[:, 512:1024], T.PK[:, 512:1024], T.b7[:], OP.add, 512)
    move("JM", "J0", T.J0[:], T.JM[:], n=16, on="v")

    for t in range(3):
        last = t == 2
        J, J2 = "J%d" % (t % 2), "J%d" % ((t + 1) % 2)
        q3, l3 = ("Q3", part("Q", 3)) if t == 0 else ("LAND%d" % t, T["LAND%d" % t][:])
        ts("JT " + J, "A32", T.A32[:], T.JT[:].indirect(T[J][:]), 4095, OP.bitwise_and, way=GATHER)
        move("A32", "A16", T.A16[:], T.A32[:])
        move("JT " + J, "NX", T.NX[:], T.JT[:].indirect(T[J][:]), 1.0 / 4096, JOB, way=GATHER)
        move("NX", "N16", T.N16[:], T.NX[:], None, -1280.0, per=0.5, on="v")
        move("A16", "AC", T.AC[:], T.A16[:], None, -1664.0, per=0.5, on="v")
        move("LM " + J, "LJ", T.LJ[:], T.LM[:].indirect(T[J][:]), way=GATHER)
        for what, mine in (("XG", VX), ("GD", VD), ("GN", VN)):
            gather(what, mine[t])
        tt("Q0 Q1", "b2h", at("b2h"), part("Q", 0), part("Q", 1), OP.max, per=2)
        tt("Q2 b2h", "b2h", at("b2h"), part("Q", 2), at("b2h"), OP.max)
        tt(q3 + " b2h", "EV", T.EV[:], l3, at("b2h"), OP.max)
        if t:
            ts(q3, "M3", part("M", 3), l3, 4095, OP.bitwise_and)
        ts("EV", "ME", T.ME[:], T.EV[:], 4095, OP.bitwise_and)
        ts("EV", "IX", T.IX[:], T.EV[:], 12, OP.logical_shift_right, 3, OP.bitwise_and)
        move("ME", "MC", T.MC[:], T.ME[:], None, -1664.0)
        move("IX", "IXB", T.IXB[:], T.IX[:])
        act("IX", "B1", T.B1[:], T.IX[:], AF.Sign, -1.5)
        if last:
            move("LAND2", "F3", T.F3[:], T.LAND2[:], 1.0 / 16384, KEY)
            move("EV", "FE", T.FE[:], T.EV[:], 1.0 / 16384, KEY)
            move("Q0 Q1 Q2", "FH", T.FH[:, 0:768], T.Q[:, 0:768], 1.0 / 16384, KEY, 768)
            add("b7h", [("NF", "F3"), ("NF", "N1K")], True, True)
            tt("LAND2 b7h", "Q3F", T.Q3F[:], T.LAND2[:], at("b7h"), OP.add)
            q3, l3 = "Q3F", T.Q3F[:]
        add("b6l", [("AVG", "BIAS")], True)
        for h in range(2):
            pick("b6l", "XG", h, "GS", lambda k: T.GS[:], h == 1)
        scan("RST b6l", "PM", T.PM[:], T.RST[:], at("b6l"), 0.0, OP.mult, OP.max)
        scan("RST PM", "PX", T.PX[:, ::-1], T.RST[:], T.PM[:, ::-1], 0.0, OP.mult, OP.max)
        tt("PX b6l", "HT", T.HT[:], T.PX[:], at("b6l"), OP.is_equal)
        for h in range(2):
            mm("HT ID", "b4l", at("b4l", 128 * h, 128 * h + 128), T.HT[:, 128 * h:128 * h + 128], T.ID[:], True, True, 128)
        move("b4l", "H", T.H[:], at("b4l"))
        for s in range(2):
            mm("ID LJ", "b3l b3h", T.b3[:, s::2], T.ID[:], T.LJ[:], True, True, 256)
        for k in range(8):
            tt(" ".join("XG%d" % c for c in range(8)) + " b3l b3h", "OV%d" % k, T.OV[:, 512 * k:512 * k + 512], T.XG[:, k::8], T.b3[:], OP.is_gt, 512)
            for s in range(2):
                for h in range(2):
                    o = 512 * k + 256 * h
                    mm("OV%d GB" % k, "b2l", at("b2l", 128 * h + k + 8 * s, 128 * h + 128, 16), T.OV[:, o + s:o + 256:2], T.GB[:], True, True, 8)
        ts("b2l", "COND", T.COND[:], at("b2l"), 8.5, OP.is_gt)
        for h in range(2):
            mm("AC ID", "b1h", at("b1h", 128 * h, 128 * h + 128), T.AC[:, 128 * h:128 * h + 128], T.ID[:], True, False, 128)
            pick("b1h", "GD", h, "ID", lambda k: T.ID[:, k::16], True)
        act("b1h", "WR", T.WR[:], at("b1h"), AF.Sign, -1407.5)
        add("b0h", [("ZERO", "ONE")], start=True)
        for h in range(2):
            pick("b0h", "GD", h, "ID", lambda k: T.ID[:, k::16], False)
        add("b0h", [("IW", "WR")], stop=True)
        tt("COND b0h", "CU", T.CU[:], T.COND[:], at("b0h"), OP.mult)
        add("b0l", [("ID", "AC"), ("IC", "ONE"), ("~IW", "COND"), ("~ID", "CU")], True, True)
        add("b3l", [("ID", "AC"), ("~IW", "COND"), ("~ID", "CU")], True, True)
        move("b3l", "UC", T.UC[:], at("b3l"))
        for i in range(4):
            tt("M%d b0l" % i, "EQ%d" % i, part("EQ", i), part("M", i), at("b0l"), OP.is_equal)
        add("b2h", [("IB", eq(i)) for i in range(4)], True, True)
        add("b5l", [("ID", "MC")], True, True)
        tt("H b5l", "G1", T.G1[:], T.H[:], at("b5l"), OP.mult)
        tt("H b2h", "HH", T.HH[:], T.H[:], at("b2h"), OP.min)
        tt("HH b3l", "G2", T.G2[:], T.HH[:], at("b3l"), OP.mult)
        tt("HH b5l", "G3", T.G3[:], T.HH[:], at("b5l"), OP.mult)
        add("b6l", [("BLK", "G1"), ("BLK", "G2"), ("NBLK", "G3")], True, True)
        add("b7l", [("ID", "MASK"), ("BLK", "G1"), ("BLK", "G2"), ("NBLK", "G3")], True, True)
        add("b4l", [("BLK", "HH")], True, True)
        move("b6l", "VR", T.VR[:], at("b6l"))
        move("b4l RS", "DL", T.DL[:], at("b4l"), T.RS[:, t:t + 1], -8.0)
        scan("CM b7l", "PV", T.PV[:], T.CM[:], at("b7l"), -4096.0, OP.max, OP.min)
        move("PV", "VL", T.VL[:], T.PV[:, 15::16], None, 1664.0, 16)
        tt("PV b6l", "E15", part("E", 15), T.PV[:], at("b6l"), OP.is_equal)
        add("b7h", [("ID", "MASK"), ("ID", "VR"), ("BLKQ", ("E15", part("E", 15)))], start=True)
        for q in range(15):
            w = slice(256 * q + 16 * q + 16, 256 * q + 256)
            ts("VR PV", "E%d" % q, T.E[:, w], T.VR[:, 16 * q + 16:256], T.PV[:, 16 * q + 15:16 * q + 16], OP.is_equal, n=240 - 16 * q, per=0.5)
            mm("BLKQ E%d" % q, "b7h", at("b7h", 16 * q + 16), T.BLKQ[:], T.E[:, w], False, q == 14, 240 - 16 * q)
        scan("CM b7h", "PO", T.PO[:], T.CM[:], at("b7h"), -4096.0, OP.max, OP.min)
        move("PO", "OL", T.OL[:], T.PO[:, 15::16], None, -2432.0, 16, on="v")
        tt("X VL DL", "Y1", T.Y1[:], T.X[:, 0:3072].indirect(T.VL[:]), T.DL[:], OP.add, way=GATHER)
        ts("Y1", "Y2", T.Y2[:], T.Y1[:], 0.0, OP.max, 255.0, OP.min, per=0.5)
        scatter("Y2 OL", "X", T.X[:].indirect(T.OL[:]), T.Y2[:])
        if last:
            D("s", "ox", "X", "YX", T.yx[:, 0:3072], T.X[:, 0:3072], 3600.0)
        for h in range(2):
            mm("NX NID", "b1l", at("b1l", 128 * h, 128 * h + 128), T.NX[:, 128 * h:128 * h + 128], T.NID[:], True, False, 128)
            pick("b1l", "GN", h, "ID", lambda k: T.ID[:, k::16], True)
        tt("COND b1l", "CN", T.CN[:], T.COND[:], at("b1l"), OP.mult)
        add("b1h", [("ID", "NX"), ("~ID", "CN")], True, True)
        move("b1h", "NN", T.NN[:], at("b1h"), None, -2304.0)
        if not last:
            add("b4h", [("ID", "NX"), ("~IK", "HT"), ("~ID", "CN")], True, True)
            act("b4h", "NH", T.NH[:], at("b4h"), AF.Relu, -2304.0)
            for r in range(16):
                mm("NH SH", "b4h", at("b4h", 0, 16), T.SH[:, 15 - r:143 - r], T.NH[:, r::16], r == 0, r == 15, 16)
            move("b4h", J2, T[J2][:], at("b4h", 0, 16), n=16)
            add("b6h", [("I4", "NN"), ("ID", "UC")], True, True)
            move("b6h", "REC", T.REC[:], at("b6h"), None, 4195968.0)
            scatter("REC " + J, "JT", T.JT[:].indirect(T[J][:]), T.REC[:])
        act("b2h", "HS", T.HS[:], at("b2h"), AF.Sign)
        t1, t2 = ("T1F", "T2F") if last else ("T1%d" % t, "T2%d" % t)
        tt(q3 + " b2h", t2, T[t2][:], l3, at("b2h"), OP.min)
        add("b0h", ([("NF", "FE"), ("NF", "N1K")] if last else []) + [("N4", "IXB"), ("NB", "HS")], True, True)
        tt("EV b0h", t1, T[t1][:], T.EV[:], at("b0h"), OP.add)
        rid, pid = topo.addr(nxt)[0:2]
        send = RemoteDMATransfer(dst_ids=[DstId(rid=rid, pnc=pid)], dma_engine_mask=topo.mask(core, nxt), remote_sem=T.sem["ar%d" % t],
                                 srcs=[T[t1][:], T[t2][:]], dsts=[T["LAND%d" % (t + 1)][:]], alu_op=2)
        call({"g": (lambda send=send, t=t: g.remote_dma_fused([send], local_sem=T.sem["lc%d" % t]), 300.0)}, t1 + " " + t2, "LAND%d" % (t + 1), 5000.0 if t else 7000.0,
             ("lc%d" % t, 0, len(topo.engines(core, nxt)), "ar%d" % t, len(topo.engines(prv, core))))
        old, new = ("b5l", "b5h", "b3l"), ("b0l", "b0h", "b3h")
        for i in range(3):
            terms = [(("ID", "NID", "ID")[i], "IXB")] + ([(("I5", "N2")[i - 1], "B1")] if i else [])
            add(old[i], terms + [("I4", eq(i)), ("NID", "HS")] + [("NB", eq(j)) for j in range(i)], True, True)
        act("b5l b5h", "SG0 SG1", T.SG[:, 0:512], T.b5[:], AF.Sign, -2.5, 512)
        act("b3l", "SG2", part("SG", 2), at("b3l"), AF.Sign, -2.5)
        for i in range(3):
            sg = ("SG%d" % i, part("SG", i))
            if last:
                add(old[i], [("NF", ("FH", part("FH", i))), ("NB", sg), ("IM", "NONE"), (("IF", "I8", "I4")[i], "NONE")], True, True)
                add(new[i], [("I4", "NN"), ("IL", sg), ("IC", sg), ("ID", "UC")], True, True)
            else:
                add(old[i], [("NB", sg)], True, True)
                add(new[i], [("IQ", "NN"), ("IB", sg), ("IP%d" % i, sg), ("ID", "UC")], True, True)
        to, op = ("OUTP", OP.add) if last else ("Q", OP.min)
        tt("Q0 Q1 b5l b5h", "TQ0", T.TQ[:, 0:512], T.Q[:, 0:512], T.b5[:], op, 512)
        tt("Q2 b3l", "TQ2", part("TQ", 2), part("Q", 2), at("b3l"), op)
        tt("TQ0 b0l b0h", to + "0 " + to + "1", T[to][:, 0:512], T.TQ[:, 0:512], T.b0[:], OP.max, 512)
        tt("TQ2 b3h", to + "2", part(to, 2), part("TQ", 2), at("b3h"), OP.max)
        if not last:
            ts("Q0 Q1 Q2", "M0 M1 M2", T.M[:, 0:768], T.Q[:, 0:768], 4095, OP.bitwise_and, n=768)
    D("s", "oq", "OUTP0 OUTP1 OUTP2", "YP", T.yp[:, 0:768], T.OUTP[:], 2600.0)
    D("a", "o3", "LAND3", "YP3", T.yp[:, 768:1024], T.LAND3[:], 2000.0)

    count = {"sv": 0, "sa": 0, "st": 0, "sg": 0}
    seen, wrote, readers = {}, {}, {}
    for i in order(calls):
        q = calls[i][0]
        R, W = ({bank(x) or x for x in tags} for tags in calls[i][3:5])
        own, need = "s" + q, {}
        for tag in R | W:
            before = [wrote[tag]] if tag in wrote else []
            before += [(s, v) for s, v in readers.get(tag, {}).items() if tag in W or bank(tag + "l") and s != own]
            for s, v in before:
                if not s == "st" == own:
                    need[s] = max(need.get(s, 0), v)
        for s in sorted(need):
            if seen.get((q, s), 0) < need[s]:
                queue[q].wait_ge(T.sem[s], need[s])
                seen[(q, s)] = need[s]
        ins = calls[i][1]()
        if i not in signals:
            count[own] += 1
        sem, inc, total = signals[i][:3] if i in signals else (own, 1, count[own])
        if inc:
            ins.then_inc(T.sem[sem], inc)
        for tag in R:
            readers.setdefault(tag, {})[sem] = total
        for tag in W:
            wrote[tag] = tuple(signals[i][3:]) if i in signals and not inc else (sem, total)
            readers[tag] = {}
    for s in ("sv", "sa", "st", "sg"):
        g.wait_ge(T.sem[s], count[s])
    for d in DMAS:
        g.wait_ge(T.sem["d" + d], 16)
    for t in range(3):
        g.wait_ge(T.sem["lc%d" % t], len(topo.engines(core, nxt)))
        g.wait_ge(T.sem["ar%d" % t], len(topo.engines(prv, core)))
